import numpy as np, ml_dtypes
CORES = [36,164,52,180,100,228,116,244]
N = 8
import mx_ref
BF = ml_dtypes.bfloat16
def gcols(t, e):
    v = np.concatenate([t.reshape(8, 16, -1, 4), np.zeros((8, 16, 1, 4), BF)], axis=2)
    return np.ascontiguousarray(np.stack([v[g][:, e[g]] for g in range(8)])).reshape(128, -1)
def tile(rs):
    return np.stack(rs, axis=2).reshape(128, -1).astype(BF)
def cut(t, i, w=512):
    return t[:, w * i:w * i + w]
def pick(q, e):
    c = np.concatenate([q[0].reshape(128, -1, 4), np.zeros((128, 1, 4), np.uint8)], axis=1); s = np.concatenate([q[1], np.ones((16, 1), np.uint8)], axis=1)
    return (np.ascontiguousarray(c[:, e].reshape(128, -1)), np.ascontiguousarray(s[:, e]))
def join(*qs):
    return (np.concatenate([q[0] for q in qs], axis=1), np.concatenate([q[1] for q in qs], axis=1))
def put(q, e, v):
    c, s = q[0].reshape(128, -1, 4).copy(), q[1].copy(); c[:, e] = v[0].reshape(128, -1, 4); s[:, e] = v[1]
    return (c.reshape(128, -1), s)
def pk(c, s):
    return (np.ascontiguousarray(c), mx_ref.live(s))
def emit(q):
    return q[0], q[1]
def packed(v, rng):
    q = [mx_ref.quantize(np.ascontiguousarray(v[r])) for r in range(N)]
    return np.stack([a for a, b in q]), np.stack([mx_ref.plane(b, rng) for a, b in q])
def values_of_codes():
    e, c = np.zeros((128, 128, 4), np.float32), np.zeros((128, 2, 4), np.uint8)
    e[np.arange(128), np.arange(128), 0] = 1
    c[:127, :, 0] = np.arange(256).reshape(2, 128).T[:127]
    return mx_ref.matmul(mx_ref.quantize(e.reshape(128, 512).astype(BF)), (c.reshape(128, 8), np.full((16, 2), 127, np.uint8))).T.reshape(-1).astype(np.float64)
CODE_VALUE, SCALE_VALUE = values_of_codes(), 2.0 ** (np.arange(256) - 127.0)
def decode(q):
    return (CODE_VALUE[q[0]].reshape(16, 8, -1, 4) * SCALE_VALUE[q[1]][:, None, :, None] + 0.0).reshape(128, -1).astype(np.float32)
def f(rng, *shape):
    return mx_ref.flush((rng.standard_normal(shape, dtype=np.float32) * np.exp2(rng.integers(-2, 3, shape[:-1] + (1,)))).astype(BF))
def wide(rng, *shape, cols=0):
    v = rng.standard_normal(shape, dtype=np.float32) * np.exp2(rng.integers(-12, 13, shape)).astype(np.float32)
    if cols: v *= np.repeat(np.exp2(rng.integers(-cols, cols + 1, shape[:-2] + (1, shape[-1] // 4))) * (rng.random(shape[:-2] + (1, shape[-1] // 4)) > 0.0625), 4, axis=-1).astype(np.float32)
    return mx_ref.flush(v.astype(BF))
C, A, R = 192, 128, 3
def slots(s, p):
    b = s[1] > s[0]
    late = np.where(b, s[1] > p[1], s[0] > p[0])
    c = np.sort(np.where(late, C * b + np.arange(C), 2 * C), axis=1)[:, :A]
    return np.where(c < 2 * C, c, -1)
def replaced(t, e, v):
    p = np.tile(np.arange(C + 1), (8, 1))
    p[np.arange(8)[:, None], e] = C + np.arange(A)
    return gcols(np.concatenate([t, v], axis=1), p[:, :C])
def big(v, k):
    v = v.astype(np.float32) * np.float32(k)
    v[np.abs(v) < np.float32(2.0 ** -16)] = 0
    return v.astype(BF)
def weights(rng, w):
    c, p = packed(w, rng)
    return {"wc": c, "ws": p}
def numbers_of(rng):
    return {"x": big(f(rng, N, 128, 12 * C), 1), "u": np.array(f(rng, N, 128, 512)), "v": np.array(f(rng, N, 128, 512))}
def kinds(rng):
    one = [(A, 0), (A - 1, 1), (A - 1, 2), (0, A), (0, A + 1), (1, 0), (0, 0), (C // 2, C - C // 2)]
    two = [(C, 0), (0, C), (A + 1, 0), (A - 1, 0), (0, A - 1), (0, 1), (C - 1, 1), (1, C - 1)]
    n = np.zeros((N, 8, 2), int)
    o = rng.permutation(N)
    for r in range(N):
        if o[r] > 0: n[r] = rng.permutation(np.array(two if o[r] == 1 else one))
    p = np.argsort(rng.random((N, 8, C)), axis=2)
    return (p >= n[:, :, :1]).astype(int) + (p >= n[:, :, :1] + n[:, :, 1:]).astype(int)
def marks(rng):
    c = kinds(rng)
    after = np.roll(c, -1, axis=0)
    m = np.full((N, 8, 3, C), 2)
    m[:, :, 0] = np.where(c == 0, 1, np.where(c == 1, rng.integers(1, 4, c.shape), rng.integers(2, 4, c.shape)))
    m[:, :, 2] = np.where(after == 1, 3, rng.integers(1, 3, c.shape))
    return m
def passing(rng):
    w = big(f(rng, N, 128, 2048), 1).reshape(N, 8, 16, 4, 8, 16, 4)
    w[:, :, 0] = 0
    w[:, :, 8:] = 0
    w[:, :, :, :, :, 0] = 0
    w[:, :, :, :, :, 8:] = 0
    w = w.reshape(N, 128, 4, 128, 4)
    for i in range(0, 128, 8):
        for b in range(4): w[:, i, b, i, b] = 32
    return weights(rng, w.reshape(N, 128, 2048))
def requantised():
    v = (np.arange(1, 16, 2)[:, None] * 2.0 ** -np.arange(10.0, 22.0)).reshape(-1)
    t = np.zeros((128, len(v), 4), np.float32)
    t[8, :, 0] = v
    t[9, :, 0] = 255 * 2.0 ** -7
    once = decode(mx_ref.quantize(t.reshape(128, -1).astype(BF)))
    again = decode(mx_ref.quantize(once.astype(BF)))
    i = int(np.argmax(np.abs(once - again)[8, ::4]))
    return float(v[i]), float(once[8, 4 * i]), float(again[8, 4 * i])
def planted(rng, m, unit, near, fine=False):
    d = numbers_of(rng)
    p = rng.permutation(8)
    s = p % 2 * 2 - 1
    if not near: m = np.where(s[:, None, None] > 0, m, 4 - m)
    x = d["x"].reshape(N, 8, 16, 3, C, 4)
    x[:, :, 0] = 0
    x[:, :, 8:] = 0
    x[:, :, 0, :, :, 0] = near
    if near: x[:, :, 0, 0, :, 0] = np.where(np.roll(m[:, :, 2], 1, axis=0) == 3, s[:, None] * 2.0 ** 28, 1.0).astype(np.float32).astype(BF)
    for b in range(3): x[:, :, 8, :, :, b] = ((m >> b & 1) * 2.0 ** b * unit).astype(np.float32).astype(BF)
    if fine:
        for g in range(8):
            if p[g] < 4:
                x[:, g, 8] = 0
                x[:, g, 8, :, :, 0] = ((4 + m[:, g]) * 2.0 ** -32).astype(np.float32).astype(BF)
        v, once, again = requantised()
        for h in (5, 7):
            g, j = int(np.argmax(p == h)), int(rng.integers(A))
            x[:, g, 8, :, j] = 0
            x[:, g, 8, 0, j, 0] = BF(min(once, again))
            x[:, g, 8, 1, j, 0] = BF(v)
            x[:, g, 9, 1, j, 0] = BF(255 * 2.0 ** -7)
    u = d["u"].reshape(N, 128, 128, 4)
    u[:, :, ::16] = 0
    k = np.where(rng.permutation(N) < N // 2, 2.0 ** -30, 1.0)
    for g in range(8):
        u[:, 16 * g, 16 * g, 0] = (k * s[g]).astype(np.float32).astype(BF)
        u[:, 16 * g + 8, 16 * g, :3] = (k * (1 if near else s[g])).astype(np.float32).astype(BF)[:, None]
    return {"x": x.reshape(N, 128, 12 * C), "u": u.reshape(N, 128, 512), "v": d["v"], **passing(rng)}
def setup_inputs(rng):
    return {**numbers_of(rng), **weights(rng, f(rng, N, 128, 2048))}
def setup_inputs_counts(rng):
    return planted(rng, marks(rng), 1.0, 0)
def setup_inputs_ties(rng):
    return planted(rng, rng.integers(0, 4, (N, 8, 3, C)), 2.0 ** -24, 0, True)
def setup_inputs_near(rng):
    return planted(rng, marks(rng), 2.0 ** -23, 1)
def setup_inputs_huge(rng):
    d = numbers_of(rng)
    x = 2.0 ** 28 * (1.5 + 0.5 * rng.random((N, 128, 12 * C)))
    x[int(rng.integers(N))] *= 2
    u = d["u"].reshape(N, 128, 128, 4)
    s = np.stack([rng.permutation(8) % 2 * 2.0 - 1.0 for r in range(N)])
    u[:, :, ::16] = (2.0 ** 30 * (0.75 + 0.25 * rng.random((N, 128, 8, 4))) * s[:, None, :, None]).astype(np.float32).astype(BF)
    w = np.zeros((N, 128, 4, 128, 4), np.float32)
    i = np.arange(128)
    for b in range(4): w[:, i, b, i, b] = 32
    return {"x": x.astype(np.float32).astype(BF), "u": u.reshape(N, 128, 512), "v": d["v"], **weights(rng, w.reshape(N, 128, 2048).astype(BF))}
def setup_inputs_spread(rng):
    d = setup_inputs(rng)
    d["x"] = big(wide(rng, N, 128, 12 * C, cols=6), 1)
    return d
def check_inputs(d):
    b = []
    for k in ("x", "u", "v"):
        a = np.abs(d[k].astype(np.float32))
        if not (np.isfinite(a).all() and ((a == 0) | (a >= 2.0 ** -30) & (a <= 2.0 ** 30)).all()): b.append("a value of " + k)
    return b
def reference(x, u, v, wc, ws):
    lay = [pk(wc[r], ws[r]) for r in range(N)]
    qu = [mx_ref.quantize(u[r]) for r in range(N)]
    level = [[np.ascontiguousarray(cut(x[r], k, 4 * C)) for k in range(3)] for r in range(N)]
    first = [mx_ref.matmul(qu[r], mx_ref.quantize(level[r][0]))[::16] for r in range(N)]
    y, ol = np.zeros((N, 128, C), np.float32), np.zeros((N, 8, R * A), np.float32)
    oc, osc = np.zeros((N, 128, 4 * C), np.uint8), np.zeros((N, 16, C), np.uint8)
    for t in range(R):
        held = [[mx_ref.quantize(level[r][k]) for k in (1, 2)] for r in range(N)]
        for r in range(N):
            log = [decode(q).astype(BF) for q in held[(r - 1) % N]]
            s = [mx_ref.matmul(qu[r], mx_ref.quantize(g))[::16] for g in log]
            p = [first[r], mx_ref.matmul(qu[r], held[r][0])[::16]]
            c = slots(s, p)
            ol[r][:, A * t:A * t + A] = c
            e = np.where(c < 0, -1, c % C)
            for k in (0, 1):
                z = (gcols(level[r][k], e).astype(np.float32) + gcols(log[k], e).astype(np.float32)) * np.float32(0.5)
                q = mx_ref.quantize(z.astype(BF))
                made = tile([np.maximum(mx_ref.matmul(pick(lay[r], np.arange(128 * a, 128 * a + 128)), q), np.float32(0.0)) * np.float32(0.03125) for a in range(4)])
                level[r][k + 1] = replaced(level[r][k + 1], np.where(c < C * k + C, e, -1), made)
    for r in range(N):
        q = mx_ref.quantize(level[r][2])
        y[r] = mx_ref.matmul(mx_ref.quantize(v[r]), q)
        oc[r], osc[r] = emit(q)
    return {"y": y, "ol": ol, "oc": oc, "osc": osc}

@@ -1,0 +1,339 @@
+from concourse.mybir import dt, AluOpType, ActivationFunctionType
+
+ALU, ACT = AluOpType, ActivationFunctionType
+C, A, R, N = 192, 128, 3, 8
+F16, BF, F32, I32, U16, U8 = "float16", "bfloat16", "float32", "int32", "uint16", "uint8"
+BIG = 4096.0
+HOLD = 512.0
+WIN = 4 * (C + 1 + A) + 12
+TB = 4 * (C + 1)
+CW = 400
+QX = "float8_e4m3fn_x4"
+
+SCRATCH = {"pa": ("psum", [128, 2048], F32), "pb": ("psum", [128, 2048], F32)}
+for _dtype, _bufs in (
+        (BF, dict(h0=4 * C, h1=4 * C, w1h=WIN, w2a=WIN, w2b=WIN, m0=4 * C + 16, g0=4 * C, g1=4 * C + 16, g1e=4 * A,
+                  z0=4 * A, z1=4 * A, ut=512, vt=512, et=2048, jb=C, step=2 * C, nl=C, nb=C, cw=R * CW, oa=A)),
+        (QX, dict(qe=512, qw=512, qu=128, qup=128, qv=128, q0=C, qh=2 * R * C, ql=2 * R * C, qg=2 * C, qz=2 * A, qf=C)),
+        (U8, dict(se=512, sw=512, su=128, sup=128, sv=128, s0=C, sh=2 * R * C, sl=2 * R * C, sg=2 * C, sz=2 * A, sf=C)),
+        (F16, dict(kk=2 * C, ka=2 * C, kb=2 * C, kc=2 * C, m16=2 * C, m4=2 * C, fl=2 * C, cum=2 * C, xx=2 * C,
+                   e16=2 * C, e4=2 * C, e2=A, ob=A, od=A)),
+        (F32, dict(dmat=128, pf=16, c4=48, jh=48, tc=32, isl=32, p0=C, p1=C, top=C, thr=C, cn=4, ta=32, tb=32, td=32,
+                   la=96, lb=96, lc=96, olb=R * A, yb=C)),
+        (I32, dict(pint=8, jint=C, jm=2 * C)),
+        (U16, dict(offu=8, offs=12, off0=32, off1=32, lst=96))):
+    for _name, _cols in _bufs.items():
+        SCRATCH[_name] = ("sbuf", [128, _cols], _dtype)
+DMAS = ["d_h1", "d_h2", "d_u", "d_h0", "d_wc", "d_ws", "d_v", "d_out"]
+SEMAPHORES = ["cv", "cs", "cp", "cg", "sent0", "sent"] + ["arr%d" % i for i in range(2 * R)] + DMAS
+
+
+def rank_program(g, core, T, topo):
+    rank = T.rank_of(core)
+    if rank is None:
+        return
+    nxt = T.cores[(rank + 1) % N]
+    rid, pid = topo.addr(nxt, core)
+    mask = topo.mask(core, nxt)
+    engines = len(topo.engines(core, nxt))
+
+    queue = {"V": g.vector, "S": g.scalar, "P": g.tensor, "G": g, "Y": g.sync}
+    own = {"V": "cv", "S": "cs", "P": "cp", "G": "cg"}
+    count = {}
+    clock = {q: {} for q in queue}
+    writer, readers = {}, {}
+
+    def need(q, ev):
+        sem, n, seen = ev
+        if clock[q].get(sem, 0) >= n:
+            return
+        queue[q].wait_ge(T.sem[sem], n)
+        for s, m in seen.items():
+            if clock[q].get(s, 0) < m:
+                clock[q][s] = m
+        clock[q][sem] = n
+
+    def order(q, r, w):
+        evs = []
+        for k in r:
+            if k in writer:
+                evs.append(writer[k])
+            if k.startswith("ps"):
+                evs += [e for (qq, e) in readers.get(k, []) if qq != q]
+        for k in w:
+            if k in writer:
+                evs.append(writer[k])
+            evs += [e for (qq, e) in readers.get(k, [])]
+        best = {}
+        for e in evs:
+            if e[0] not in best or best[e[0]][1] < e[1]:
+                best[e[0]] = e
+        for e in sorted(best.values(), key=lambda e: -sum(e[2].values())):
+            need(q, e)
+
+    def note(q, ev, r, w):
+        for k in r:
+            readers.setdefault(k, []).append((q, ev))
+        for k in w:
+            writer[k] = ev
+            readers[k] = []
+
+    def op(q, r, w, call):
+        order(q, r, w)
+        sem = own[q]
+        count[sem] = count.get(sem, 0) + 1
+        call().then_inc(T.sem[sem], 1)
+        note(q, (sem, count[sem], dict(clock[q])), r, w)
+
+    def dma(q, sem, r, w, out, in_):
+        order(q, r, w)
+        count[sem] = count.get(sem, 0) + 16
+        queue[q].dma_start(out, in_).then_inc(T.sem[sem], 16)
+        note(q, (sem, count[sem], dict(clock[q])), r, w)
+
+    V, S, P = g.vector, g.scalar, g.tensor
+
+    def ts(r, w, out, in0, s1, op0, s2=None, op1=None):
+        if op1 is None:
+            op("V", r, w, lambda: V.tensor_scalar(out, in0, s1, None, op0))
+        else:
+            op("V", r, w, lambda: V.tensor_scalar(out, in0, s1, s2, op0, op1))
+
+    def tt(r, w, out, in0, in1, o):
+        op("V", r, w, lambda: V.tensor_tensor(out, in0, in1, o))
+
+    def scan(r, w, out, d0, d1, init, op0, op1):
+        op("V", r, w, lambda: V.tensor_tensor_scan(out, d0, d1, init, op0, op1))
+
+    def cp(r, w, out, in_):
+        op("V", r, w, lambda: V.tensor_copy(out, in_))
+
+    def fill(w, ap, c):
+        op("V", [], w, lambda: V.memset(ap, c))
+
+    def act(r, w, out, in_, func=ACT.Copy, scale=1.0):
+        if scale == 1.0:
+            op("S", r, w, lambda: S.activation(out, in_, func))
+        else:
+            op("S", r, w, lambda: S.activation(out, in_, func, scale=scale))
+
+    def quant(r, w, q, s, a, n, tile):
+        op("V", r, w, lambda: V.quantize_mx(q[:, a:a + n], s[:, a:a + n], tile))
+
+    def bank(i, n):
+        buf = T.pa if i < 4 else T.pb
+        return buf[:, 512 * (i % 4):512 * (i % 4) + n]
+
+    def mm(r, i, lq, ls, la, rq, rs, ra, n):
+        op("P", r, ["ps%d" % i], lambda: P.matmul_mx(bank(i, n), lq[:, la:la + 128], ls[:, la:la + 128],
+                                                    rq[:, ra:ra + n], rs[:, ra:ra + n], True, True))
+
+    def send(t, k):
+        i = 2 * t + k
+        a = C * i
+        order("G", ["qh%d" % i], [])
+        loc = "sent0" if t == 0 else "sent"
+        arr = T.sem["arr%d" % i]
+        g.remote_dma(T.ql[:, a:a + C].bitcast(dt.uint8), T.qh[:, a:a + C].bitcast(dt.uint8), arr, T.sem[loc], pid, rid, mask)
+        g.remote_dma(T.sl[:, a:a + C], T.sh[:, a:a + C], arr, T.sem[loc], pid, rid, mask)
+        count[loc] = count.get(loc, 0) + 2 * engines
+        count["arr%d" % i] = 2 * engines
+        writer["ql%d" % i] = ("arr%d" % i, 2 * engines, {})
+
+    four = lambda name: ["%s.%d" % (name, b) for b in range(4)]
+    pf = lambda i: T.pf[:, i:i + 1]
+    RR, TT, QQ, H16, H4, CA, C191, C320 = range(8)
+
+    dma("Y", "d_h1", [], ["h1"], T.h1[:], T.x[:, 4 * C:8 * C])
+    dma("Y", "d_h2", [], ["w2a.l0", "w2a.l1"], T.w2a[:, 0:4 * C], T.x[:, 8 * C:12 * C])
+    dma("Y", "d_u", [], ["ut"], T.ut[:], T.u[:])
+    dma("Y", "d_h0", [], ["h0"], T.h0[:], T.x[:, 0:4 * C])
+
+    op("G", [], ["dmat"], lambda: g.iota(T.dmat[:], [[1, 128]], 0, -1, allow_small_or_imprecise_dtypes=True))
+    op("G", [], ["pi"], lambda: g.iota(T.pint[:, 0:1], [[1, 1]], 0, 1))
+    op("G", [], ["jint"], lambda: g.iota(T.jint[:], [[1, C]], 0, 0))
+    op("G", [], ["c4"], lambda: g.iota(T.c4[:], [[4, 48]], 0, 0, allow_small_or_imprecise_dtypes=True))
+    fill(four("et"), T.et[:], 0.0)
+    fill(["w1h.z"], T.w1h[:, 4 * C:TB], 0.0)
+    fill(["m0.z"], T.m0[:, 4 * C:], 0.0)
+    fill(["g1.z"], T.g1[:, 4 * C:], 0.0)
+    for b in range(4):
+        ts(["dmat"], ["et.%d" % b], T.et[:, 512 * b + b:512 * b + 512:4], T.dmat[:], 0.0, ALU.is_equal)
+    ts(["pi"], ["pi1"], T.pint[:, 1:2], T.pint[:, 0:1], 15, ALU.bitwise_and)
+    ts(["pi"], ["pi2"], T.pint[:, 2:3], T.pint[:, 0:1], 3, ALU.bitwise_and)
+    ts(["pi"], ["pi3"], T.pint[:, 3:4], T.pint[:, 0:1], 2, ALU.logical_shift_right, 3, ALU.bitwise_and)
+    ts(["jint"], ["jm.0"], T.jm[:, 0:C], T.jint[:], 15, ALU.bitwise_and)
+    cp(["pi1", "pi2", "pi3"], ["pf"], T.pf[:, 0:3], T.pint[:, 1:4])
+    ts(["jint"], ["jm.1"], T.jm[:, C:2 * C], T.jint[:], 3, ALU.bitwise_and)
+    ts(["c4"], ["offu"], T.offu[:], T.c4[:, 0:8], 4.0, ALU.mult)
+
+    quant(["h1"], ["qh0"], T.qh, T.sh, 0, C, T.h1[:])
+    send(0, 0)
+    act(["h1"], ["w1h.l"], T.w1h[:, 0:4 * C], T.h1[:], scale=0.5)
+    quant(["w2a.l0", "w2a.l1"], ["qh1"], T.qh, T.sh, C, C, T.w2a[:, 0:4 * C])
+    send(0, 1)
+    need("Y", ("sent0", count["sent0"], {}))
+    dma("Y", "d_wc", [], ["qw"], T.qw[:].bitcast(dt.uint8), T.wc[:])
+    dma("Y", "d_ws", [], ["sw"], T.sw[:], T.ws[:])
+    dma("Y", "d_v", [], ["vt"], T.vt[:], T.v[:])
+
+    quant(four("et"), ["qe"], T.qe, T.se, 0, 512, T.et[:])
+    quant(["ut"], ["qu"], T.qu, T.su, 0, 128, T.ut[:])
+    ts(["jm.0", "pf"], ["kk.0"], T.kk[:, 0:C], T.jm[:, 0:C], pf(RR), ALU.subtract)
+    cp(["qu", "offu"], ["qup"], T.qup[:, 0:128].bitcast(dt.uint32), T.qu[:, 0:128].bitcast(dt.uint32).indirect(T.offu[:, 0:8]))
+    act(["qu", "offu"], ["sup"], T.sup[:, 0:128], T.su[:, 0:128].indirect(T.offu[:, 0:8]))
+    quant(["h0"], ["q0"], T.q0, T.s0, 0, C, T.h0[:])
+    mm(["qup", "sup", "qh0"], 2, T.qup, T.sup, 0, T.qh, T.sh, 0, C)
+    mm(["qup", "sup", "q0"], 3, T.qup, T.sup, 0, T.q0, T.s0, 0, C)
+    act(["ps2"], ["p1"], T.p1[:], bank(2, C))
+    act(["ps3"], ["p0"], T.p0[:], bank(3, C))
+    ts(["jm.1", "pf"], ["kk.1"], T.kk[:, C:2 * C], T.jm[:, C:2 * C], pf(QQ), ALU.subtract)
+    cp(["jint"], ["jb"], T.jb[:], T.jint[:])
+    ts(["pf"], ["h16"], pf(H16), pf(RR), 15.0, ALU.is_lt, HOLD, ALU.mult)
+    ts(["pf"], ["h4"], pf(H4), pf(QQ), 3.0, ALU.is_lt, HOLD, ALU.mult)
+    ts(["kk.0", "kk.1"], ["ka"], T.ka[:], T.kk[:], 2048.0, ALU.mult, 0.0, ALU.min)
+    ts(["kk.0", "kk.1"], ["kb"], T.kb[:], T.kk[:], 0.0, ALU.is_equal, HOLD, ALU.mult)
+    ts(["h4", "pf"], ["ca"], pf(CA), pf(H4), -4.0, ALU.mult, pf(TT), ALU.add)
+    ts(["h4"], ["c191"], pf(C191), pf(H4), float(C - 1), ALU.add)
+    ts(["h4"], ["c320"], pf(C320), pf(H4), float(C + A), ALU.add)
+    ts(["c4", "pf", "h4"], ["jh"], T.jh[:], T.c4[:], pf(QQ), ALU.add, pf(H4), ALU.add)
+    ts(["c4", "pf"], ["isl"], T.isl[:], T.c4[:, 0:32], pf(QQ), ALU.add, 1.0, ALU.add)
+    tt(["ka", "kb"], ["kc"], T.kc[:], T.ka[:], T.kb[:], ALU.add)
+    ts(["jh"], ["tc"], T.tc[:], T.jh[:, 0:32], float(C + 1), ALU.add)
+    fill(["cw0", "cw1", "cw2"], T.cw[:], float(C))
+    fill(["step.0"], T.step[:, 0:C], 1.0)
+    fill(["step.1"], T.step[:, C:C + 1], float(1 - C))
+    fill(["step.2"], T.step[:, C + 1:], 0.0)
+    fill(["w2a.z"], T.w2a[:, 4 * C:TB], 0.0)
+    fill(["w2b.z"], T.w2b[:, 4 * C:TB], 0.0)
+    cp(["kc"], ["m16.e"], T.m16[:, 2:2 * C:2], T.kc[:, 0:C - 1])
+    cp(["kc"], ["m4.e"], T.m4[:, 2:2 * C:2], T.kc[:, C:2 * C - 1])
+    tt(["kc", "jb"], ["m16.o"], T.m16[:, 1:2 * C:2], T.kc[:, 0:C], T.jb[:], ALU.min)
+    ts(["jb"], ["m16.e"], T.m16[:, 0:2 * C:32], T.jb[:, 0:12], 0.0, ALU.mult, -2048.0, ALU.add)
+    ts(["jb"], ["m4.e"], T.m4[:, 0:2 * C:8], T.jb[:, 0:48], 0.0, ALU.mult, -2048.0, ALU.add)
+    tt(["kc", "jb"], ["m4.o"], T.m4[:, 1:2 * C:2], T.kc[:, C:2 * C], T.jb[:], ALU.min)
+
+    def ol_a(t):
+        ts(["jb", "cn"], ["oa"], T.oa[:], T.jb[:, 1:A + 1], T.cn[:, 0:1], ALU.is_ge, float(C), ALU.mult)
+
+    def ol_b(t):
+        tt(["oa", "cw%d" % t], ["ob"], T.ob[:], T.oa[:], T.cw[:, CW * t + C + 1:CW * t + C + 1 + A], ALU.add)
+
+    def ol_c(t):
+        ts(["ob"], ["od"], T.od[:], T.ob[:], float(2 * C), ALU.is_ge, float(-2 * C - 1), ALU.mult)
+
+    def ol_d(t):
+        tt(["ob", "od"], ["olb%d" % t], T.olb[:, A * t:A * t + A], T.ob[:], T.od[:], ALU.add)
+
+    def list_steps(k, limit, limit_key):
+        raw = T.e4[:, 7:2 * C:8]
+        sl = slice(48 * k, 48 * k + 48)
+        return [
+            lambda: ts(["e4", limit_key], ["la%d" % k], T.la[:, sl], raw, limit, ALU.is_gt, -BIG, ALU.mult),
+            lambda: tt(["e4", "la%d" % k], ["lb%d" % k], T.lb[:, sl], raw, T.la[:, sl], ALU.add),
+            lambda: tt(["lb%d" % k, "jh"], ["lc%d" % k], T.lc[:, sl], T.lb[:, sl], T.jh[:], ALU.max),
+            lambda: ts(["lc%d" % k, "ca"], ["lst%d" % k], T.lst[:, sl], T.lc[:, sl], 4.0, ALU.mult, pf(CA), ALU.add),
+        ]
+
+    for t in range(R):
+        last = t == R - 1
+        wn, wo = ("w2a", "w2b") if t % 2 == 0 else ("w2b", "w2a")
+        W2, W2o = T[wn], T[wo]
+        a0, a1 = C * 2 * t, C * (2 * t + 1)
+        for b in range(4):
+            mm(["qe", "ql%d" % (2 * t)], b, T.qe, T.se, 128 * b, T.ql, T.sl, a0, C)
+        for b in range(4):
+            act(["ps%d" % b], ["g0.%d" % b], T.g0[:, b:4 * C:4], bank(b, C))
+        for b in range(4):
+            if b == 3:
+                quant(four("g0"), ["qg0"], T.qg, T.sg, 0, C, T.g0[:])
+            tt(["ps%d" % b, "h0"], ["m0.%d" % b], T.m0[:, b:4 * C:4], bank(b, C), T.h0[:, b:4 * C:4], ALU.add)
+        mm(["qup", "sup", "qg0"], 0, T.qup, T.sup, 0, T.qg, T.sg, 0, C)
+        for b in range(4):
+            mm(["qe", "ql%d" % (2 * t + 1)], 4 + b, T.qe, T.se, 128 * b, T.ql, T.sl, a1, C)
+        tt(["ps0", "p0"], ["nl"], T.nl[:], bank(0, C), T.p0[:], ALU.is_le)
+        tt(["ps0", "p1"], ["top"], T.top[:], bank(0, C), T.p1[:], ALU.max)
+        ts(["nl"], ["nb"], T.nb[:], T.nl[:], -1e29, ALU.mult)
+        tt(["ps0", "nb"], ["thr"], T.thr[:], bank(0, C), T.nb[:], ALU.add)
+        for b in range(4):
+            act(["ps%d" % (4 + b)], ["g1.%d" % b], T.g1[:, b:4 * C:4], bank(4 + b, C))
+        quant(four("g1"), ["qg1"], T.qg, T.sg, C, C, T.g1[:, 0:4 * C])
+        mm(["qup", "sup", "qg1"], 1, T.qup, T.sup, 0, T.qg, T.sg, C, C)
+        tt(["ps1", "thr"], ["fl.0"], T.fl[:, 0:C], bank(1, C), T.thr[:], ALU.is_le)
+        tt(["ps1", "top"], ["fl.1"], T.fl[:, C:2 * C], bank(1, C), T.top[:], ALU.is_gt)
+        scan(["fl.0", "fl.1", "step.0", "step.1", "step.2"], ["cum"], T.cum[:], T.fl[:], T.step[:], float(C + 1), ALU.add, ALU.subtract)
+        scan(["cum", "fl.0"], ["xx.0"], T.xx[:, 0:2 * C:2], T.cum[:, 0:C], T.fl[:, 0:C], 0.0, ALU.max, ALU.mult)
+        scan(["cum", "fl.1"], ["xx.1"], T.xx[:, 1:2 * C:2], T.cum[:, C:2 * C], T.fl[:, C:2 * C], 0.0, ALU.max, ALU.mult)
+        cp(["cum"], ["cn"], T.cn[:, 0:1], T.cum[:, C - 1:C])
+        scan(["xx.0", "xx.1", "m16.e", "m16.o"], ["e16"], T.e16[:], T.m16[:], T.xx[:], 0.0, ALU.add, ALU.max)
+        ts(["isl", "cn"], ["ta"], T.ta[:], T.isl[:], T.cn[:, 0:1], ALU.is_lt, BIG, ALU.mult)
+        ts(["e16", "h16"], ["offs"], T.offs[:], T.e16[:, 31:2 * C:32], pf(H16), ALU.subtract)
+        if not last:
+            ts(["cn", "c191", "c320"], ["lim"], T.cn[:, 1:2], T.cn[:, 0:1], pf(C191), ALU.add, pf(C320), ALU.min)
+        cp(["offs", "jb"], ["cw%d" % t], T.cw[:, CW * t:CW * t + CW].indirect(T.offs[:, 0:12]), T.jb[:])
+        tt(["ta", "tc"], ["tb"], T.tb[:], T.ta[:], T.tc[:], ALU.min)
+        scan(["cw%d" % t, "m4.e"], ["e2"], T.e2[:], T.m4[:, 0:2 * A:2], T.cw[:, CW * t + C + 1:CW * t + C + 1 + A], 0.0, ALU.add, ALU.max)
+        ts(["e2", "ca"], ["off0"], T.off0[:], T.e2[:, 3:A:4], 4.0, ALU.mult, pf(CA), ALU.add)
+        mw = four("m0") + ["m0.z", "off0"]
+        act(mw, ["z0.1"], T.z0[:, 256:512], T.m0[:].indirect(T.off0[:, 16:32]), scale=0.5)
+        ts(mw, ["z0.0"], T.z0[:, 0:256], T.m0[:].indirect(T.off0[:, 0:16]), 0.5, ALU.mult)
+        act(four("g1") + ["g1.z", "off0"], ["g1e"], T.g1e[:], T.g1[:].indirect(T.off0[:, 0:32]), scale=0.5)
+        tt(["tb", "e2"], ["td"], T.td[:], T.tb[:], T.e2[:, 3:A:4], ALU.max)
+        quant(["z0.0", "z0.1"], ["qz0"], T.qz, T.sz, 0, A, T.z0[:])
+        for a in range(4):
+            mm(["qw", "sw", "qz0"], 4 + a, T.qw, T.sw, 128 * a, T.qz, T.sz, 0, A)
+        scan(["xx.0", "xx.1", "m4.e", "m4.o"], ["e4"], T.e4[:], T.m4[:], T.xx[:], 0.0, ALU.add, ALU.max)
+        ts(["td", "ca"], ["off1"], T.off1[:], T.td[:], 4.0, ALU.mult, pf(CA), ALU.add)
+        extra = [lambda: ol_a(t), lambda: ol_b(t), lambda: None, lambda: None] if last else list_steps(0, T.cn[:, 1:2], "lim")
+        extra[0]()
+        for a in range(3):
+            ts(["ps%d" % (4 + a)], ["w1h.t%d" % a], T.w1h[:, TB + a:TB + 4 * A:4], bank(4 + a, A), 0.0, ALU.max, 2.0 ** -6, ALU.mult)
+            extra[a + 1]()
+        act(["ps7"], ["w1h.t3"], T.w1h[:, TB + 3:TB + 4 * A:4], bank(7, A), ACT.Relu, 2.0 ** -6)
+        w1 = ["w1h.l", "w1h.z"] + ["w1h.t%d" % a for a in range(4)]
+        tt(w1 + ["off1", "g1e"], ["z1"], T.z1[:], T.w1h[:, 0:TB + 4 * A].indirect(T.off1[:, 0:32]), T.g1e[:], ALU.add)
+        if not last:
+            act(w1 + ["lst0"], ["h1"], T.h1[:], T.w1h[:, 0:TB + 4 * A].indirect(T.lst[:, 0:48]), scale=2.0)
+        quant(["z1"], ["qz1"], T.qz, T.sz, A, A, T.z1[:])
+        for a in range(4):
+            mm(["qw", "sw", "qz1"], 4 + a, T.qw, T.sw, 128 * a, T.qz, T.sz, A, A)
+        for step in list_steps(1, pf(C320), "c320"):
+            step()
+        if not last:
+            quant(["h1"], ["qh%d" % (2 * t + 2)], T.qh, T.sh, a0 + 2 * C, C, T.h1[:])
+            send(t + 1, 0)
+            mm(["qup", "sup", "qh%d" % (2 * t + 2)], 2, T.qup, T.sup, 0, T.qh, T.sh, a0 + 2 * C, C)
+        else:
+            ol_c(t)
+            ol_d(t)
+            dma("Y", "d_out", ["olb0", "olb1", "olb2"], [], T.ol[:], T.olb[0:128:16, :])
+        for a in range(2):
+            act(["ps%d" % (4 + a)], ["%s.t%d" % (wn, a)], W2[:, TB + a:TB + 4 * A:4], bank(4 + a, A), ACT.Relu, 2.0 ** -5)
+        for a in range(2, 4):
+            ts(["ps%d" % (4 + a)], ["%s.t%d" % (wn, a)], W2[:, TB + a:TB + 4 * A:4], bank(4 + a, A), 0.0, ALU.max, 2.0 ** -5, ALU.mult)
+        w2 = [wn + ".l0", wn + ".l1", wn + ".z", "lst1"] + ["%s.t%d" % (wn, a) for a in range(4)]
+        act(w2, [wo + ".l1"], W2o[:, 2 * C:4 * C], W2[:, 0:TB + 4 * A].indirect(T.lst[:, 72:96]))
+        cp(w2, [wo + ".l0"], W2o[:, 0:2 * C], W2[:, 0:TB + 4 * A].indirect(T.lst[:, 48:72]))
+        if not last:
+            quant([wo + ".l0", wo + ".l1"], ["qh%d" % (2 * t + 3)], T.qh, T.sh, a1 + 2 * C, C, W2o[:, 0:4 * C])
+            send(t + 1, 1)
+            act(["ps2"], ["p1"], T.p1[:], bank(2, C))
+            act(["h1"], ["w1h.l"], T.w1h[:, 0:4 * C], T.h1[:], scale=0.5)
+            ol_a(t)
+            if t == 0:
+                quant(["vt"], ["qv"], T.qv, T.sv, 0, 128, T.vt[:])
+            ol_b(t)
+            ol_c(t)
+            ol_d(t)
+        else:
+            quant([wo + ".l0", wo + ".l1"], ["qf"], T.qf, T.sf, 0, C, W2o[:, 0:4 * C])
+            mm(["qv", "qf"], 0, T.qv, T.sv, 0, T.qf, T.sf, 0, C)
+            dma("Y", "d_out", ["qf"], [], T.oc[:], T.qf[:].bitcast(dt.uint8))
+            for k in range(4):
+                dma("Y" if k < 2 else "S", "d_out", ["qf"], [], T.osc[4 * k:4 * k + 4, :], T.sf[32 * k:32 * k + 4, :])
+            cp(["ps0"], ["yb"], T.yb[:], bank(0, C))
+            dma("S", "d_out", ["yb"], [], T.y[:], T.yb[:])
+
+    for sem in SEMAPHORES:
+        if count.get(sem, 0):
+            g.wait_ge(T.sem[sem], count[sem])

@@ -13,11 +13,11 @@ QX = "float8_e4m3fn_x4"
 SCRATCH = {"pa": ("psum", [128, 2048], F32), "pb": ("psum", [128, 2048], F32)}
 for _dtype, _bufs in (
         (BF, dict(h0=4 * C, h1=4 * C, w1h=WIN, w2a=WIN, w2b=WIN, m0=4 * C + 16, g0=4 * C, g1=4 * C + 16, g1e=4 * A,
-                  z0=4 * A, z1=4 * A, ut=512, vt=512, et=2048, jb=C, step=2 * C, nl=C, nb=C, cw=R * CW, oa=A)),
+                  z0=4 * A, z1=4 * A, ut=512, vt=512, et=2048, jb=C, step=2 * C, nl=C, nb=C, cw=R * CW, oa=A,
+                  kk=2 * C, ka=2 * C, kb=2 * C, kc=2 * C, m16=2 * C, m4=2 * C)),
         (QX, dict(qe=512, qw=512, qu=128, qup=128, qv=128, q0=C, qh=2 * R * C, ql=2 * R * C, qg=2 * C, qz=2 * A, qf=C)),
         (U8, dict(se=512, sw=512, su=128, sup=128, sv=128, s0=C, sh=2 * R * C, sl=2 * R * C, sg=2 * C, sz=2 * A, sf=C)),
-        (F16, dict(kk=2 * C, ka=2 * C, kb=2 * C, kc=2 * C, m16=2 * C, m4=2 * C, fl=2 * C, cum=2 * C, xx=2 * C,
-                   e16=2 * C, e4=2 * C, e2=A, ob=A, od=A)),
+        (F16, dict(fl=2 * C, cum=2 * C, xx=2 * C, e16=2 * C, e4=2 * C, e2=A, ob=A, od=A)),
         (F32, dict(dmat=128, pf=16, c4=48, jh=48, tc=32, isl=32, p0=C, p1=C, top=C, thr=C, cn=4, ta=32, tb=32, td=32,
                    la=96, lb=96, lc=96, olb=R * A, yb=C)),
         (I32, dict(pint=8, jint=C, jm=2 * C)),
@@ -117,6 +117,12 @@ def rank_program(g, core, T, topo):
         else:
             op("S", r, w, lambda: S.activation(out, in_, func, scale=scale))
 
+    def iota(w, out, step, n, base, per_partition, whole=False):
+        if whole:
+            op("G", [], w, lambda: g.iota(out, [[step, n]], base, per_partition))
+        else:
+            op("G", [], w, lambda: g.iota(out, [[step, n]], base, per_partition, allow_small_or_imprecise_dtypes=True))
+
     def quant(r, w, q, s, a, n, tile):
         op("V", r, w, lambda: V.quantize_mx(q[:, a:a + n], s[:, a:a + n], tile))
 
@@ -143,87 +149,89 @@ def rank_program(g, core, T, topo):
     four = lambda name: ["%s.%d" % (name, b) for b in range(4)]
     pf = lambda i: T.pf[:, i:i + 1]
     RR, TT, QQ, H16, H4, CA, C191, C320 = range(8)
+    ET = ["et.%d.%d" % (b, e) for b in range(4) for e in range(4)]
 
     dma("Y", "d_h1", [], ["h1"], T.h1[:], T.x[:, 4 * C:8 * C])
     dma("Y", "d_h2", [], ["w2a.l0", "w2a.l1"], T.w2a[:, 0:4 * C], T.x[:, 8 * C:12 * C])
     dma("Y", "d_u", [], ["ut"], T.ut[:], T.u[:])
     dma("Y", "d_h0", [], ["h0"], T.h0[:], T.x[:, 0:4 * C])
 
-    op("G", [], ["dmat"], lambda: g.iota(T.dmat[:], [[1, 128]], 0, -1, allow_small_or_imprecise_dtypes=True))
-    op("G", [], ["pi"], lambda: g.iota(T.pint[:, 0:1], [[1, 1]], 0, 1))
-    op("G", [], ["jint"], lambda: g.iota(T.jint[:], [[1, C]], 0, 0))
-    op("G", [], ["c4"], lambda: g.iota(T.c4[:], [[4, 48]], 0, 0, allow_small_or_imprecise_dtypes=True))
-    fill(four("et"), T.et[:], 0.0)
+    iota(["pi"], T.pint[:, 0:1], 1, 1, 0, 1, True)
+    iota(["dmat"], T.dmat[:], 1, 128, 0, -1)
+    iota(["jint"], T.jint[:], 1, C, 0, 0, True)
+    iota(["c4"], T.c4[:], 4, 48, 0, 0)
     fill(["w1h.z"], T.w1h[:, 4 * C:TB], 0.0)
     fill(["m0.z"], T.m0[:, 4 * C:], 0.0)
     fill(["g1.z"], T.g1[:, 4 * C:], 0.0)
-    for b in range(4):
-        ts(["dmat"], ["et.%d" % b], T.et[:, 512 * b + b:512 * b + 512:4], T.dmat[:], 0.0, ALU.is_equal)
+    fill(["w2a.z"], T.w2a[:, 4 * C:TB], 0.0)
+    fill(["w2b.z"], T.w2b[:, 4 * C:TB], 0.0)
     ts(["pi"], ["pi1"], T.pint[:, 1:2], T.pint[:, 0:1], 15, ALU.bitwise_and)
     ts(["pi"], ["pi2"], T.pint[:, 2:3], T.pint[:, 0:1], 3, ALU.bitwise_and)
     ts(["pi"], ["pi3"], T.pint[:, 3:4], T.pint[:, 0:1], 2, ALU.logical_shift_right, 3, ALU.bitwise_and)
-    ts(["jint"], ["jm.0"], T.jm[:, 0:C], T.jint[:], 15, ALU.bitwise_and)
+    fill(["step.0"], T.step[:, 0:C], 1.0)
+    fill(["step.1"], T.step[:, C:C + 1], float(1 - C))
+    fill(["step.2"], T.step[:, C + 1:], 0.0)
     cp(["pi1", "pi2", "pi3"], ["pf"], T.pf[:, 0:3], T.pint[:, 1:4])
+    for b in range(4):
+        ts(["dmat"], ["et.%d.%d" % (b, b)], T.et[:, 512 * b + b:512 * b + 512:4], T.dmat[:], 0.0, ALU.is_equal)
+        for e in range(4):
+            if e != b:
+                act(["dmat"], ["et.%d.%d" % (b, e)], T.et[:, 512 * b + e:512 * b + 512:4], T.dmat[:], scale=0.0)
+    ts(["pf"], ["h4"], pf(H4), pf(QQ), 3.0, ALU.is_lt, HOLD, ALU.mult)
+    ts(["pf"], ["h16"], pf(H16), pf(RR), 15.0, ALU.is_lt, HOLD, ALU.mult)
+    ts(["jint"], ["jm.0"], T.jm[:, 0:C], T.jint[:], 15, ALU.bitwise_and)
     ts(["jint"], ["jm.1"], T.jm[:, C:2 * C], T.jint[:], 3, ALU.bitwise_and)
     ts(["c4"], ["offu"], T.offu[:], T.c4[:, 0:8], 4.0, ALU.mult)
+    ts(["jm.0", "pf"], ["kk.0"], T.kk[:, 0:C], T.jm[:, 0:C], pf(RR), ALU.subtract)
+    ts(["jm.1", "pf"], ["kk.1"], T.kk[:, C:2 * C], T.jm[:, C:2 * C], pf(QQ), ALU.subtract)
 
     quant(["h1"], ["qh0"], T.qh, T.sh, 0, C, T.h1[:])
     send(0, 0)
-    act(["h1"], ["w1h.l"], T.w1h[:, 0:4 * C], T.h1[:], scale=0.5)
+    act(["kk.0", "kk.1"], ["ka"], T.ka[:], T.kk[:], ACT.Relu, -2048.0)
+    ts(["kk.0", "kk.1"], ["kb"], T.kb[:], T.kk[:], 0.0, ALU.is_equal, HOLD, ALU.mult)
+    cp(["jint"], ["jb"], T.jb[:], T.jint[:])
     quant(["w2a.l0", "w2a.l1"], ["qh1"], T.qh, T.sh, C, C, T.w2a[:, 0:4 * C])
     send(0, 1)
+    for t in range(R):
+        iota(["cw%d" % t], T.cw[:, CW * t:CW * t + CW], 0, CW, C, 0)
     need("Y", ("sent0", count["sent0"], {}))
     dma("Y", "d_wc", [], ["qw"], T.qw[:].bitcast(dt.uint8), T.wc[:])
     dma("Y", "d_ws", [], ["sw"], T.sw[:], T.ws[:])
     dma("Y", "d_v", [], ["vt"], T.vt[:], T.v[:])
 
-    quant(four("et"), ["qe"], T.qe, T.se, 0, 512, T.et[:])
     quant(["ut"], ["qu"], T.qu, T.su, 0, 128, T.ut[:])
-    ts(["jm.0", "pf"], ["kk.0"], T.kk[:, 0:C], T.jm[:, 0:C], pf(RR), ALU.subtract)
-    cp(["qu", "offu"], ["qup"], T.qup[:, 0:128].bitcast(dt.uint32), T.qu[:, 0:128].bitcast(dt.uint32).indirect(T.offu[:, 0:8]))
+    quant(ET, ["qe"], T.qe, T.se, 0, 512, T.et[:])
     act(["qu", "offu"], ["sup"], T.sup[:, 0:128], T.su[:, 0:128].indirect(T.offu[:, 0:8]))
+    cp(["qu", "offu"], ["qup"], T.qup[:, 0:128].bitcast(dt.uint32), T.qu[:, 0:128].bitcast(dt.uint32).indirect(T.offu[:, 0:8]))
     quant(["h0"], ["q0"], T.q0, T.s0, 0, C, T.h0[:])
+    act(["h1"], ["w1h.l"], T.w1h[:, 0:4 * C], T.h1[:], scale=0.5)
     mm(["qup", "sup", "qh0"], 2, T.qup, T.sup, 0, T.qh, T.sh, 0, C)
     mm(["qup", "sup", "q0"], 3, T.qup, T.sup, 0, T.q0, T.s0, 0, C)
+    tt(["ka", "kb"], ["kc"], T.kc[:], T.kb[:], T.ka[:], ALU.subtract)
     act(["ps2"], ["p1"], T.p1[:], bank(2, C))
     act(["ps3"], ["p0"], T.p0[:], bank(3, C))
-    ts(["jm.1", "pf"], ["kk.1"], T.kk[:, C:2 * C], T.jm[:, C:2 * C], pf(QQ), ALU.subtract)
-    cp(["jint"], ["jb"], T.jb[:], T.jint[:])
-    ts(["pf"], ["h16"], pf(H16), pf(RR), 15.0, ALU.is_lt, HOLD, ALU.mult)
-    ts(["pf"], ["h4"], pf(H4), pf(QQ), 3.0, ALU.is_lt, HOLD, ALU.mult)
-    ts(["kk.0", "kk.1"], ["ka"], T.ka[:], T.kk[:], 2048.0, ALU.mult, 0.0, ALU.min)
-    ts(["kk.0", "kk.1"], ["kb"], T.kb[:], T.kk[:], 0.0, ALU.is_equal, HOLD, ALU.mult)
     ts(["h4", "pf"], ["ca"], pf(CA), pf(H4), -4.0, ALU.mult, pf(TT), ALU.add)
-    ts(["h4"], ["c191"], pf(C191), pf(H4), float(C - 1), ALU.add)
-    ts(["h4"], ["c320"], pf(C320), pf(H4), float(C + A), ALU.add)
     ts(["c4", "pf", "h4"], ["jh"], T.jh[:], T.c4[:], pf(QQ), ALU.add, pf(H4), ALU.add)
-    ts(["c4", "pf"], ["isl"], T.isl[:], T.c4[:, 0:32], pf(QQ), ALU.add, 1.0, ALU.add)
-    tt(["ka", "kb"], ["kc"], T.kc[:], T.ka[:], T.kb[:], ALU.add)
-    ts(["jh"], ["tc"], T.tc[:], T.jh[:, 0:32], float(C + 1), ALU.add)
-    fill(["cw0", "cw1", "cw2"], T.cw[:], float(C))
-    fill(["step.0"], T.step[:, 0:C], 1.0)
-    fill(["step.1"], T.step[:, C:C + 1], float(1 - C))
-    fill(["step.2"], T.step[:, C + 1:], 0.0)
-    fill(["w2a.z"], T.w2a[:, 4 * C:TB], 0.0)
-    fill(["w2b.z"], T.w2b[:, 4 * C:TB], 0.0)
     cp(["kc"], ["m16.e"], T.m16[:, 2:2 * C:2], T.kc[:, 0:C - 1])
     cp(["kc"], ["m4.e"], T.m4[:, 2:2 * C:2], T.kc[:, C:2 * C - 1])
     tt(["kc", "jb"], ["m16.o"], T.m16[:, 1:2 * C:2], T.kc[:, 0:C], T.jb[:], ALU.min)
     ts(["jb"], ["m16.e"], T.m16[:, 0:2 * C:32], T.jb[:, 0:12], 0.0, ALU.mult, -2048.0, ALU.add)
     ts(["jb"], ["m4.e"], T.m4[:, 0:2 * C:8], T.jb[:, 0:48], 0.0, ALU.mult, -2048.0, ALU.add)
-    tt(["kc", "jb"], ["m4.o"], T.m4[:, 1:2 * C:2], T.kc[:, C:2 * C], T.jb[:], ALU.min)
+    late_constants = [
+        lambda: tt(["kc", "jb"], ["m4.o"], T.m4[:, 1:2 * C:2], T.kc[:, C:2 * C], T.jb[:], ALU.min),
+        lambda: ts(["h4"], ["c191"], pf(C191), pf(H4), float(C - 1), ALU.add),
+        lambda: ts(["h4"], ["c320"], pf(C320), pf(H4), float(C + A), ALU.add),
+        lambda: ts(["c4", "pf"], ["isl"], T.isl[:], T.c4[:, 0:32], pf(QQ), ALU.add, 1.0, ALU.add),
+        lambda: ts(["jh"], ["tc"], T.tc[:], T.jh[:, 0:32], float(C + 1), ALU.add),
+    ]
 
-    def ol_a(t):
-        ts(["jb", "cn"], ["oa"], T.oa[:], T.jb[:, 1:A + 1], T.cn[:, 0:1], ALU.is_ge, float(C), ALU.mult)
-
-    def ol_b(t):
-        tt(["oa", "cw%d" % t], ["ob"], T.ob[:], T.oa[:], T.cw[:, CW * t + C + 1:CW * t + C + 1 + A], ALU.add)
-
-    def ol_c(t):
-        ts(["ob"], ["od"], T.od[:], T.ob[:], float(2 * C), ALU.is_ge, float(-2 * C - 1), ALU.mult)
-
-    def ol_d(t):
-        tt(["ob", "od"], ["olb%d" % t], T.olb[:, A * t:A * t + A], T.ob[:], T.od[:], ALU.add)
+    def ol_steps(t):
+        return [
+            lambda: ts(["jb", "cn"], ["oa"], T.oa[:], T.jb[:, 1:A + 1], T.cn[:, 0:1], ALU.is_ge, float(C), ALU.mult),
+            lambda: tt(["oa", "cw%d" % t], ["ob"], T.ob[:], T.oa[:], T.cw[:, CW * t + C + 1:CW * t + C + 1 + A], ALU.add),
+            lambda: ts(["ob"], ["od"], T.od[:], T.ob[:], float(2 * C), ALU.is_ge, float(-2 * C - 1), ALU.mult),
+            lambda: tt(["ob", "od"], ["olb%d" % t], T.olb[:, A * t:A * t + A], T.ob[:], T.od[:], ALU.add),
+        ]
 
     def list_steps(k, limit, limit_key):
         raw = T.e4[:, 7:2 * C:8]
@@ -244,72 +252,94 @@ def rank_program(g, core, T, topo):
             mm(["qe", "ql%d" % (2 * t)], b, T.qe, T.se, 128 * b, T.ql, T.sl, a0, C)
         for b in range(4):
             act(["ps%d" % b], ["g0.%d" % b], T.g0[:, b:4 * C:4], bank(b, C))
-        for b in range(4):
-            if b == 3:
-                quant(four("g0"), ["qg0"], T.qg, T.sg, 0, C, T.g0[:])
-            tt(["ps%d" % b, "h0"], ["m0.%d" % b], T.m0[:, b:4 * C:4], bank(b, C), T.h0[:, b:4 * C:4], ALU.add)
+        sums = [(lambda b=b: tt(["ps%d" % b, "h0"], ["m0.%d" % b], T.m0[:, b:4 * C:4], bank(b, C), T.h0[:, b:4 * C:4], ALU.add))
+                for b in range(4)]
+        sums[0]()
+        sums[1]()
+        quant(four("g0"), ["qg0"], T.qg, T.sg, 0, C, T.g0[:])
         mm(["qup", "sup", "qg0"], 0, T.qup, T.sup, 0, T.qg, T.sg, 0, C)
+        sums[2]()
         for b in range(4):
             mm(["qe", "ql%d" % (2 * t + 1)], 4 + b, T.qe, T.se, 128 * b, T.ql, T.sl, a1, C)
         tt(["ps0", "p0"], ["nl"], T.nl[:], bank(0, C), T.p0[:], ALU.is_le)
         tt(["ps0", "p1"], ["top"], T.top[:], bank(0, C), T.p1[:], ALU.max)
         ts(["nl"], ["nb"], T.nb[:], T.nl[:], -1e29, ALU.mult)
-        tt(["ps0", "nb"], ["thr"], T.thr[:], bank(0, C), T.nb[:], ALU.add)
+        sums[3]()
         for b in range(4):
             act(["ps%d" % (4 + b)], ["g1.%d" % b], T.g1[:, b:4 * C:4], bank(4 + b, C))
         quant(four("g1"), ["qg1"], T.qg, T.sg, C, C, T.g1[:, 0:4 * C])
         mm(["qup", "sup", "qg1"], 1, T.qup, T.sup, 0, T.qg, T.sg, C, C)
-        tt(["ps1", "thr"], ["fl.0"], T.fl[:, 0:C], bank(1, C), T.thr[:], ALU.is_le)
+        tt(["ps0", "nb"], ["thr"], T.thr[:], bank(0, C), T.nb[:], ALU.add)
+        if t == 0:
+            late_constants[0]()
+        l2 = list_steps(1, pf(C320), "c320")
+        l1 = ol_steps(t) if last else list_steps(0, T.cn[:, 1:2], "lim")
         tt(["ps1", "top"], ["fl.1"], T.fl[:, C:2 * C], bank(1, C), T.top[:], ALU.is_gt)
+        tt(["ps1", "thr"], ["fl.0"], T.fl[:, 0:C], bank(1, C), T.thr[:], ALU.is_le)
+        if t == 0:
+            late_constants[1]()
+            late_constants[2]()
         scan(["fl.0", "fl.1", "step.0", "step.1", "step.2"], ["cum"], T.cum[:], T.fl[:], T.step[:], float(C + 1), ALU.add, ALU.subtract)
+        if t == 0:
+            late_constants[3]()
+            late_constants[4]()
         scan(["cum", "fl.0"], ["xx.0"], T.xx[:, 0:2 * C:2], T.cum[:, 0:C], T.fl[:, 0:C], 0.0, ALU.max, ALU.mult)
         scan(["cum", "fl.1"], ["xx.1"], T.xx[:, 1:2 * C:2], T.cum[:, C:2 * C], T.fl[:, C:2 * C], 0.0, ALU.max, ALU.mult)
         cp(["cum"], ["cn"], T.cn[:, 0:1], T.cum[:, C - 1:C])
         scan(["xx.0", "xx.1", "m16.e", "m16.o"], ["e16"], T.e16[:], T.m16[:], T.xx[:], 0.0, ALU.add, ALU.max)
-        ts(["isl", "cn"], ["ta"], T.ta[:], T.isl[:], T.cn[:, 0:1], ALU.is_lt, BIG, ALU.mult)
+        scan(["xx.0", "xx.1", "m4.e", "m4.o"], ["e4"], T.e4[:], T.m4[:], T.xx[:], 0.0, ALU.add, ALU.max)
         ts(["e16", "h16"], ["offs"], T.offs[:], T.e16[:, 31:2 * C:32], pf(H16), ALU.subtract)
         if not last:
             ts(["cn", "c191", "c320"], ["lim"], T.cn[:, 1:2], T.cn[:, 0:1], pf(C191), ALU.add, pf(C320), ALU.min)
+        ts(["isl", "cn"], ["ta"], T.ta[:], T.isl[:], T.cn[:, 0:1], ALU.is_lt, BIG, ALU.mult)
         cp(["offs", "jb"], ["cw%d" % t], T.cw[:, CW * t:CW * t + CW].indirect(T.offs[:, 0:12]), T.jb[:])
+        l1[0]()
         tt(["ta", "tc"], ["tb"], T.tb[:], T.ta[:], T.tc[:], ALU.min)
         scan(["cw%d" % t, "m4.e"], ["e2"], T.e2[:], T.m4[:, 0:2 * A:2], T.cw[:, CW * t + C + 1:CW * t + C + 1 + A], 0.0, ALU.add, ALU.max)
+        if last:
+            l2[0]()
+        else:
+            l1[1]()
         ts(["e2", "ca"], ["off0"], T.off0[:], T.e2[:, 3:A:4], 4.0, ALU.mult, pf(CA), ALU.add)
+        tt(["tb", "e2"], ["td"], T.td[:], T.tb[:], T.e2[:, 3:A:4], ALU.max)
         mw = four("m0") + ["m0.z", "off0"]
         act(mw, ["z0.1"], T.z0[:, 256:512], T.m0[:].indirect(T.off0[:, 16:32]), scale=0.5)
         ts(mw, ["z0.0"], T.z0[:, 0:256], T.m0[:].indirect(T.off0[:, 0:16]), 0.5, ALU.mult)
         act(four("g1") + ["g1.z", "off0"], ["g1e"], T.g1e[:], T.g1[:].indirect(T.off0[:, 0:32]), scale=0.5)
-        tt(["tb", "e2"], ["td"], T.td[:], T.tb[:], T.e2[:, 3:A:4], ALU.max)
+        ts(["td", "ca"], ["off1"], T.off1[:], T.td[:], 4.0, ALU.mult, pf(CA), ALU.add)
+        (l2[1] if last else l1[2])()
         quant(["z0.0", "z0.1"], ["qz0"], T.qz, T.sz, 0, A, T.z0[:])
         for a in range(4):
             mm(["qw", "sw", "qz0"], 4 + a, T.qw, T.sw, 128 * a, T.qz, T.sz, 0, A)
-        scan(["xx.0", "xx.1", "m4.e", "m4.o"], ["e4"], T.e4[:], T.m4[:], T.xx[:], 0.0, ALU.add, ALU.max)
-        ts(["td", "ca"], ["off1"], T.off1[:], T.td[:], 4.0, ALU.mult, pf(CA), ALU.add)
-        extra = [lambda: ol_a(t), lambda: ol_b(t), lambda: None, lambda: None] if last else list_steps(0, T.cn[:, 1:2], "lim")
-        extra[0]()
+        if last:
+            l1[1]()
+            l2[2]()
+        else:
+            l1[3]()
+            l2[0]()
         for a in range(3):
             ts(["ps%d" % (4 + a)], ["w1h.t%d" % a], T.w1h[:, TB + a:TB + 4 * A:4], bank(4 + a, A), 0.0, ALU.max, 2.0 ** -6, ALU.mult)
-            extra[a + 1]()
         act(["ps7"], ["w1h.t3"], T.w1h[:, TB + 3:TB + 4 * A:4], bank(7, A), ACT.Relu, 2.0 ** -6)
+        (l1[2] if last else l2[1])()
         w1 = ["w1h.l", "w1h.z"] + ["w1h.t%d" % a for a in range(4)]
         tt(w1 + ["off1", "g1e"], ["z1"], T.z1[:], T.w1h[:, 0:TB + 4 * A].indirect(T.off1[:, 0:32]), T.g1e[:], ALU.add)
         if not last:
             act(w1 + ["lst0"], ["h1"], T.h1[:], T.w1h[:, 0:TB + 4 * A].indirect(T.lst[:, 0:48]), scale=2.0)
+        (l2[3] if last else l2[2])()
         quant(["z1"], ["qz1"], T.qz, T.sz, A, A, T.z1[:])
         for a in range(4):
             mm(["qw", "sw", "qz1"], 4 + a, T.qw, T.sw, 128 * a, T.qz, T.sz, A, A)
-        for step in list_steps(1, pf(C320), "c320"):
-            step()
         if not last:
+            l2[3]()
             quant(["h1"], ["qh%d" % (2 * t + 2)], T.qh, T.sh, a0 + 2 * C, C, T.h1[:])
             send(t + 1, 0)
             mm(["qup", "sup", "qh%d" % (2 * t + 2)], 2, T.qup, T.sup, 0, T.qh, T.sh, a0 + 2 * C, C)
         else:
-            ol_c(t)
-            ol_d(t)
+            l1[3]()
             dma("Y", "d_out", ["olb0", "olb1", "olb2"], [], T.ol[:], T.olb[0:128:16, :])
-        for a in range(2):
+        for a in ((0, 2) if last else (0, 1)):
             act(["ps%d" % (4 + a)], ["%s.t%d" % (wn, a)], W2[:, TB + a:TB + 4 * A:4], bank(4 + a, A), ACT.Relu, 2.0 ** -5)
-        for a in range(2, 4):
+        for a in ((1, 3) if last else (2, 3)):
             ts(["ps%d" % (4 + a)], ["%s.t%d" % (wn, a)], W2[:, TB + a:TB + 4 * A:4], bank(4 + a, A), 0.0, ALU.max, 2.0 ** -5, ALU.mult)
         w2 = [wn + ".l0", wn + ".l1", wn + ".z", "lst1"] + ["%s.t%d" % (wn, a) for a in range(4)]
         act(w2, [wo + ".l1"], W2o[:, 2 * C:4 * C], W2[:, 0:TB + 4 * A].indirect(T.lst[:, 72:96]))
@@ -319,12 +349,12 @@ def rank_program(g, core, T, topo):
             send(t + 1, 1)
             act(["ps2"], ["p1"], T.p1[:], bank(2, C))
             act(["h1"], ["w1h.l"], T.w1h[:, 0:4 * C], T.h1[:], scale=0.5)
-            ol_a(t)
+            steps = ol_steps(t)
+            steps[0]()
             if t == 0:
                 quant(["vt"], ["qv"], T.qv, T.sv, 0, 128, T.vt[:])
-            ol_b(t)
-            ol_c(t)
-            ol_d(t)
+            for step in steps[1:]:
+                step()
         else:
             quant([wo + ".l0", wo + ".l1"], ["qf"], T.qf, T.sf, 0, C, W2o[:, 0:4 * C])
             mm(["qv", "qf"], 0, T.qv, T.sv, 0, T.qf, T.sf, 0, C)

@@ -4,28 +4,35 @@ ALU, ACT = AluOpType, ActivationFunctionType
 C, A, R, N = 192, 128, 3, 8
 F16, BF, F32, I32, U16, U8 = "float16", "bfloat16", "float32", "int32", "uint16", "uint8"
 BIG = 4096.0
-HOLD = 512.0
-WIN = 4 * (C + 1 + A) + 12
-TB = 4 * (C + 1)
-CW = 400
+HOLD, LIFT = 512.0, 1024.0
+NIL = C + A
+W1 = NIL + 16
+W2 = C + R * A
+WG = C + (R - 1) * A
+P0 = 2 * C - 1
+CW = P0 + 1 + C
+SENT = 2 * C + 2 * (R - 1) * A
+LW = 24
 QX = "float8_e4m3fn_x4"
 
 SCRATCH = {"pa": ("psum", [128, 2048], F32), "pb": ("psum", [128, 2048], F32)}
 for _dtype, _bufs in (
-        (BF, dict(h0=4 * C, h1=4 * C, w1h=WIN, w2a=WIN, w2b=WIN, m0=4 * C + 16, g0=4 * C, g1=4 * C + 16, g1e=4 * A,
-                  z0=4 * A, z1=4 * A, ut=512, vt=512, et=2048, jb=C, step=2 * C, nl=C, nb=C, cw=R * CW, oa=A,
-                  kk=2 * C, ka=2 * C, kb=2 * C, kc=2 * C, m16=2 * C, m4=2 * C)),
-        (QX, dict(qe=512, qw=512, qu=128, qup=128, qv=128, q0=C, qh=2 * R * C, ql=2 * R * C, qg=2 * C, qz=2 * A, qf=C)),
-        (U8, dict(se=512, sw=512, su=128, sup=128, sv=128, s0=C, sh=2 * R * C, sl=2 * R * C, sg=2 * C, sz=2 * A, sf=C)),
-        (F16, dict(fl=2 * C, cum=2 * C, xx=2 * C, e16=2 * C, e4=2 * C, e2=A, ob=A, od=A)),
-        (F32, dict(dmat=128, pf=16, c4=48, jh=48, tc=32, isl=32, p0=C, p1=C, top=C, thr=C, cn=4, ta=32, tb=32, td=32,
-                   la=96, lb=96, lc=96, olb=R * A, yb=C)),
-        (I32, dict(pint=8, jint=C, jm=2 * C)),
-        (U16, dict(offu=8, offs=12, off0=32, off1=32, lst=96))):
+        (BF, dict(h0=4 * C, h1=4 * C, h2=4 * C, w1=4 * W1, w2=4 * W2, wg0=4 * WG, wg1=4 * WG, m0=4 * NIL + 16,
+                  m1=4 * NIL + 16, m2=4 * NIL + 16, g0=4 * C, g1=4 * NIL + 16, g1e=4 * A, z0=4 * A, z1=4 * A, t0=4 * A,
+                  t1=4 * A, ut=512, vt=512, et=520, jb=C, jm=C + 16, jr=A, one=C, nl=C, nb=C, cw=R * CW, oa=A, ka=C,
+                  kb=C + 2, m16=2 * C, m4a=A, m4=A)),
+        (QX, dict(qe=512, qw=512, qu=128, qup=128, qv=128, q0=C, q1=C, qh=SENT, ql=SENT, qg=2 * C, qz=2 * A, qf=C)),
+        (U8, dict(se=512, sw=512, su=128, sup=128, sv=128, s0=C, s1=C, sh=SENT, sl=SENT, sg=2 * C, sz=2 * A, sf=C)),
+        (F16, dict(fl=2 * C, cum0=C, cum1=C, xx=2 * C, e16=2 * C, e2=A, ob=A, od=A)),
+        (F32, dict(dmat=128, pf=16, c4=48, jc=24, pos=12, cn=2, tc=32, isl=32, p0=C, p1=C, top=C, thr=C, lim=2, ta=32,
+                   tb=32, td=32, la=24, lb=24, lf=24, lg=24, lh=24, cur=24, olb=R * A, yb=C)),
+        (I32, dict(pint=8)),
+        (U16, dict(offu=8, offs=12, off0=32, off1=32, lown=12, ls=LW * R, rl=LW * (R - 1)))):
     for _name, _cols in _bufs.items():
         SCRATCH[_name] = ("sbuf", [128, _cols], _dtype)
-DMAS = ["d_h1", "d_h2", "d_u", "d_h0", "d_wc", "d_ws", "d_v", "d_out"]
-SEMAPHORES = ["cv", "cs", "cp", "cg", "sent0", "sent"] + ["arr%d" % i for i in range(2 * R)] + DMAS
+DMAS = ["d_h1", "d_h2", "d_u", "d_h0", "d_wc", "d_ws", "d_v", "d_m1", "d_m2", "d_add", "d_out"]
+SEMAPHORES = (["cv", "cs", "cp", "cg", "sent0", "sent"] + ["arr%d" % i for i in range(2 * R)]
+              + ["arl%d" % i for i in range(R - 1)] + DMAS)
 
 
 def rank_program(g, core, T, topo):
@@ -85,10 +92,10 @@ def rank_program(g, core, T, topo):
         call().then_inc(T.sem[sem], 1)
         note(q, (sem, count[sem], dict(clock[q])), r, w)
 
-    def dma(q, sem, r, w, out, in_):
+    def dma(q, sem, r, w, out, in_, **how):
         order(q, r, w)
         count[sem] = count.get(sem, 0) + 16
-        queue[q].dma_start(out, in_).then_inc(T.sem[sem], 16)
+        queue[q].dma_start(out, in_, **how).then_inc(T.sem[sem], 16)
         note(q, (sem, count[sem], dict(clock[q])), r, w)
 
     V, S, P = g.vector, g.scalar, g.tensor
@@ -117,11 +124,25 @@ def rank_program(g, core, T, topo):
         else:
             op("S", r, w, lambda: S.activation(out, in_, func, scale=scale))
 
-    def iota(w, out, step, n, base, per_partition, whole=False):
-        if whole:
-            op("G", [], w, lambda: g.iota(out, [[step, n]], base, per_partition))
+    def move(q, r, w, out, in_, scale=1.0):
+        if q == "S":
+            act(r, w, out, in_, scale=scale)
+        elif scale == 1.0:
+            cp(r, w, out, in_)
         else:
-            op("G", [], w, lambda: g.iota(out, [[step, n]], base, per_partition, allow_small_or_imprecise_dtypes=True))
+            ts(r, w, out, in_, scale, ALU.mult)
+
+    def relu(q, r, w, out, in_, scale):
+        if q == "S":
+            act(r, w, out, in_, ACT.Relu, scale)
+        else:
+            ts(r, w, out, in_, 0.0, ALU.max, scale, ALU.mult)
+
+    def iota(w, out, pattern, base, per_partition, whole=False):
+        if whole:
+            op("G", [], w, lambda: g.iota(out, pattern, base, per_partition))
+        else:
+            op("G", [], w, lambda: g.iota(out, pattern, base, per_partition, allow_small_or_imprecise_dtypes=True))
 
     def quant(r, w, q, s, a, n, tile):
         op("V", r, w, lambda: V.quantize_mx(q[:, a:a + n], s[:, a:a + n], tile))
@@ -134,229 +155,279 @@ def rank_program(g, core, T, topo):
         op("P", r, ["ps%d" % i], lambda: P.matmul_mx(bank(i, n), lq[:, la:la + 128], ls[:, la:la + 128],
                                                     rq[:, ra:ra + n], rs[:, ra:ra + n], True, True))
 
+    def piece(t, k):
+        return (C * k, C) if t == 0 else (2 * C + A * (2 * t - 2 + k), A)
+
+    def remote(key, arr, loc, lands, pairs):
+        order("G", [key], [])
+        for out, in_ in pairs:
+            g.remote_dma(out, in_, T.sem[arr], T.sem[loc], pid, rid, mask)
+        count[loc] = count.get(loc, 0) + len(pairs) * engines
+        count[arr] = len(pairs) * engines
+        writer[lands] = (arr, count[arr], {})
+
     def send(t, k):
         i = 2 * t + k
-        a = C * i
-        order("G", ["qh%d" % i], [])
-        loc = "sent0" if t == 0 else "sent"
-        arr = T.sem["arr%d" % i]
-        g.remote_dma(T.ql[:, a:a + C].bitcast(dt.uint8), T.qh[:, a:a + C].bitcast(dt.uint8), arr, T.sem[loc], pid, rid, mask)
-        g.remote_dma(T.sl[:, a:a + C], T.sh[:, a:a + C], arr, T.sem[loc], pid, rid, mask)
-        count[loc] = count.get(loc, 0) + 2 * engines
-        count["arr%d" % i] = 2 * engines
-        writer["ql%d" % i] = ("arr%d" % i, 2 * engines, {})
+        a, n = piece(t, k)
+        remote("qh%d" % i, "arr%d" % i, "sent0" if t == 0 else "sent", "ql%d" % i,
+               [(T.ql[:, a:a + n].bitcast(dt.uint8), T.qh[:, a:a + n].bitcast(dt.uint8)), (T.sl[:, a:a + n], T.sh[:, a:a + n])])
 
     four = lambda name: ["%s.%d" % (name, b) for b in range(4)]
     pf = lambda i: T.pf[:, i:i + 1]
-    RR, TT, QQ, H16, H4, CA, C191, C320 = range(8)
-    ET = ["et.%d.%d" % (b, e) for b in range(4) for e in range(4)]
+    Q16, T4, R4, H16, H4, CA0, CA1, LA, LB, LC, HC = range(11)
+    cn = T.cn[:, 0:1]
+    PAIR = "SVSV"
 
-    dma("Y", "d_h1", [], ["h1"], T.h1[:], T.x[:, 4 * C:8 * C])
-    dma("Y", "d_h2", [], ["w2a.l0", "w2a.l1"], T.w2a[:, 0:4 * C], T.x[:, 8 * C:12 * C])
+    dma("Y", "d_h1", [], four("h1"), T.h1[:], T.x[:, 4 * C:8 * C])
+    dma("Y", "d_h2", [], four("h2"), T.h2[:], T.x[:, 8 * C:12 * C])
     dma("Y", "d_u", [], ["ut"], T.ut[:], T.u[:])
     dma("Y", "d_h0", [], ["h0"], T.h0[:], T.x[:, 0:4 * C])
 
-    iota(["pi"], T.pint[:, 0:1], 1, 1, 0, 1, True)
-    iota(["dmat"], T.dmat[:], 1, 128, 0, -1)
-    iota(["jint"], T.jint[:], 1, C, 0, 0, True)
-    iota(["c4"], T.c4[:], 4, 48, 0, 0)
-    fill(["w1h.z"], T.w1h[:, 4 * C:TB], 0.0)
-    fill(["m0.z"], T.m0[:, 4 * C:], 0.0)
-    fill(["g1.z"], T.g1[:, 4 * C:], 0.0)
-    fill(["w2a.z"], T.w2a[:, 4 * C:TB], 0.0)
-    fill(["w2b.z"], T.w2b[:, 4 * C:TB], 0.0)
+    iota(["dmat"], T.dmat[:], [[1, 128]], 0, -1)
+    iota(["pi"], T.pint[:, 0:1], [[1, 1]], 0, 1, True)
+    iota(["c4"], T.c4[:], [[4, 48]], 0, 0)
+    iota(["jm"], T.jm[:], [[0, 13], [1, 16]], 0, 0)
+    iota(["jb"], T.jb[:], [[1, C]], 0, 0)
+    fill(["et"], T.et[:], 0.0)
+    fill(["one"], T.one[:], 1.0)
+    ts(["dmat"], ["et"], T.et[:, 3:515:4], T.dmat[:], 0.0, ALU.is_equal)
     ts(["pi"], ["pi1"], T.pint[:, 1:2], T.pint[:, 0:1], 15, ALU.bitwise_and)
     ts(["pi"], ["pi2"], T.pint[:, 2:3], T.pint[:, 0:1], 3, ALU.bitwise_and)
     ts(["pi"], ["pi3"], T.pint[:, 3:4], T.pint[:, 0:1], 2, ALU.logical_shift_right, 3, ALU.bitwise_and)
-    fill(["step.0"], T.step[:, 0:C], 1.0)
-    fill(["step.1"], T.step[:, C:C + 1], float(1 - C))
-    fill(["step.2"], T.step[:, C + 1:], 0.0)
-    cp(["pi1", "pi2", "pi3"], ["pf"], T.pf[:, 0:3], T.pint[:, 1:4])
     for b in range(4):
-        ts(["dmat"], ["et.%d.%d" % (b, b)], T.et[:, 512 * b + b:512 * b + 512:4], T.dmat[:], 0.0, ALU.is_equal)
-        for e in range(4):
-            if e != b:
-                act(["dmat"], ["et.%d.%d" % (b, e)], T.et[:, 512 * b + e:512 * b + 512:4], T.dmat[:], scale=0.0)
-    ts(["pf"], ["h4"], pf(H4), pf(QQ), 3.0, ALU.is_lt, HOLD, ALU.mult)
-    ts(["pf"], ["h16"], pf(H16), pf(RR), 15.0, ALU.is_lt, HOLD, ALU.mult)
-    ts(["jint"], ["jm.0"], T.jm[:, 0:C], T.jint[:], 15, ALU.bitwise_and)
-    ts(["jint"], ["jm.1"], T.jm[:, C:2 * C], T.jint[:], 3, ALU.bitwise_and)
+        quant(["et"], ["qe%d" % b], T.qe, T.se, 128 * b, 128, T.et[:, 3 - b:515 - b])
+        if b == 0:
+            cp(["pi1", "pi2", "pi3"], ["pf"], T.pf[:, 0:3], T.pint[:, 1:4])
     ts(["c4"], ["offu"], T.offu[:], T.c4[:, 0:8], 4.0, ALU.mult)
-    ts(["jm.0", "pf"], ["kk.0"], T.kk[:, 0:C], T.jm[:, 0:C], pf(RR), ALU.subtract)
-    ts(["jm.1", "pf"], ["kk.1"], T.kk[:, C:2 * C], T.jm[:, C:2 * C], pf(QQ), ALU.subtract)
+    ts(["pf"], ["h4"], pf(H4), pf(R4), -HOLD, ALU.mult, 3 * HOLD, ALU.add)
+    ts(["pf"], ["h16"], pf(H16), pf(Q16), 15.0, ALU.is_lt, LIFT, ALU.mult)
 
-    quant(["h1"], ["qh0"], T.qh, T.sh, 0, C, T.h1[:])
+    def halves_of_h1():
+        for b in range(4):
+            move("S", ["h1.%d" % b], ["w1.l%d" % b], T.w1[:, W1 * b:W1 * b + C], T.h1[:, b:4 * C:4], 0.5)
+
+    def round_constants(t):
+        iota(["cw%d" % t], T.cw[:, CW * t:CW * t + CW], [[0, CW]], NIL, 0)
+        if t > 0:
+            iota(["m%d.z" % t], T["m%d" % t][:, 4 * C:], [[0, 4 * A + 16]], 0, 0)
+
+    quant(four("h1"), ["qh0"], T.qh, T.sh, 0, C, T.h1[:])
     send(0, 0)
-    act(["kk.0", "kk.1"], ["ka"], T.ka[:], T.kk[:], ACT.Relu, -2048.0)
-    ts(["kk.0", "kk.1"], ["kb"], T.kb[:], T.kk[:], 0.0, ALU.is_equal, HOLD, ALU.mult)
-    cp(["jint"], ["jb"], T.jb[:], T.jint[:])
-    quant(["w2a.l0", "w2a.l1"], ["qh1"], T.qh, T.sh, C, C, T.w2a[:, 0:4 * C])
+    ts(["jm", "pf"], ["kb"], T.kb[:, 0:C + 1], T.jm[:, 15:C + 16], pf(Q16), ALU.is_equal, LIFT, ALU.mult)
+    halves_of_h1()
+    quant(four("h2"), ["qh1"], T.qh, T.sh, C, C, T.h2[:])
     send(0, 1)
-    for t in range(R):
-        iota(["cw%d" % t], T.cw[:, CW * t:CW * t + CW], 0, CW, C, 0)
+    iota(["jr"], T.jr[:], [[0, A // 4], [1, 4]], 0, 0)
+    round_constants(0)
+    round_constants(1)
     need("Y", ("sent0", count["sent0"], {}))
     dma("Y", "d_wc", [], ["qw"], T.qw[:].bitcast(dt.uint8), T.wc[:])
     dma("Y", "d_ws", [], ["sw"], T.sw[:], T.ws[:])
-    dma("Y", "d_v", [], ["vt"], T.vt[:], T.v[:])
+    for t in range(1, R):
+        dma("Y", "d_m%d" % t, [], four("m%d" % t), T["m%d" % t][:, 0:4 * C], T.x[:, 0:4 * C])
+    dma("G", "d_v", ["qw", "sw"], ["vt"], T.vt[:], T.v[:])
 
     quant(["ut"], ["qu"], T.qu, T.su, 0, 128, T.ut[:])
-    quant(ET, ["qe"], T.qe, T.se, 0, 512, T.et[:])
+    act(["kb"], ["ka"], T.ka[:], T.kb[:, 1:C + 1], scale=-2.0)
+    tt(["kb", "jb"], ["m16.o"], T.m16[:, 1:2 * C:2], T.kb[:, 1:C + 1], T.jb[:], ALU.min)
     act(["qu", "offu"], ["sup"], T.sup[:, 0:128], T.su[:, 0:128].indirect(T.offu[:, 0:8]))
     cp(["qu", "offu"], ["qup"], T.qup[:, 0:128].bitcast(dt.uint32), T.qu[:, 0:128].bitcast(dt.uint32).indirect(T.offu[:, 0:8]))
     quant(["h0"], ["q0"], T.q0, T.s0, 0, C, T.h0[:])
-    act(["h1"], ["w1h.l"], T.w1h[:, 0:4 * C], T.h1[:], scale=0.5)
-    mm(["qup", "sup", "qh0"], 2, T.qup, T.sup, 0, T.qh, T.sh, 0, C)
-    mm(["qup", "sup", "q0"], 3, T.qup, T.sup, 0, T.q0, T.s0, 0, C)
-    tt(["ka", "kb"], ["kc"], T.kc[:], T.kb[:], T.ka[:], ALU.subtract)
-    act(["ps2"], ["p1"], T.p1[:], bank(2, C))
-    act(["ps3"], ["p0"], T.p0[:], bank(3, C))
-    ts(["h4", "pf"], ["ca"], pf(CA), pf(H4), -4.0, ALU.mult, pf(TT), ALU.add)
-    ts(["c4", "pf", "h4"], ["jh"], T.jh[:], T.c4[:], pf(QQ), ALU.add, pf(H4), ALU.add)
-    cp(["kc"], ["m16.e"], T.m16[:, 2:2 * C:2], T.kc[:, 0:C - 1])
-    cp(["kc"], ["m4.e"], T.m4[:, 2:2 * C:2], T.kc[:, C:2 * C - 1])
-    tt(["kc", "jb"], ["m16.o"], T.m16[:, 1:2 * C:2], T.kc[:, 0:C], T.jb[:], ALU.min)
-    ts(["jb"], ["m16.e"], T.m16[:, 0:2 * C:32], T.jb[:, 0:12], 0.0, ALU.mult, -2048.0, ALU.add)
-    ts(["jb"], ["m4.e"], T.m4[:, 0:2 * C:8], T.jb[:, 0:48], 0.0, ALU.mult, -2048.0, ALU.add)
-    late_constants = [
-        lambda: tt(["kc", "jb"], ["m4.o"], T.m4[:, 1:2 * C:2], T.kc[:, C:2 * C], T.jb[:], ALU.min),
-        lambda: ts(["h4"], ["c191"], pf(C191), pf(H4), float(C - 1), ALU.add),
-        lambda: ts(["h4"], ["c320"], pf(C320), pf(H4), float(C + A), ALU.add),
-        lambda: ts(["c4", "pf"], ["isl"], T.isl[:], T.c4[:, 0:32], pf(QQ), ALU.add, 1.0, ALU.add),
-        lambda: ts(["jh"], ["tc"], T.tc[:], T.jh[:, 0:32], float(C + 1), ALU.add),
-    ]
+    mm(["qup", "sup", "qh0"], 4, T.qup, T.sup, 0, T.qh, T.sh, 0, C)
+    mm(["qup", "sup", "q0"], 5, T.qup, T.sup, 0, T.q0, T.s0, 0, C)
+    act(["ps4"], ["p1"], T.p1[:], bank(4, C))
+    act(["ps5"], ["p0"], T.p0[:], bank(5, C))
+    tt(["ka", "kb"], ["m16.e"], T.m16[:, 0:2 * C:2], T.ka[:], T.kb[:, 0:C], ALU.add)
+    ts(["jr", "pf"], ["m4a"], T.m4a[:], T.jr[:], pf(R4), ALU.is_equal, -BIG - HOLD, ALU.mult)
+    ts(["h4", "pf"], ["ca0"], pf(CA0), pf(H4), -4.0, ALU.mult, pf(T4), ALU.add)
+    ts(["h4", "pf"], ["ca1"], pf(CA1), pf(T4), float(W1), ALU.mult, pf(H4), ALU.subtract)
+    for i, c in ((LA, A - 1), (LB, P0), (LC, P0 + A), (HC, C)):
+        ts(["h16"], ["pf%d" % i], pf(i), pf(H16), float(c), ALU.add)
+    ts(["m4a"], ["m4"], T.m4[:], T.m4a[:], HOLD, ALU.add)
+    for k in range(2):
+        ts(["c4", "pf"], ["jc%d" % k], T.jc[:, 12 * k:12 * k + 12], T.c4[:, 0:48:4], pf(Q16), ALU.add)
+    ts(["c4", "pf"], ["isl"], T.isl[:], T.c4[:, 0:32], pf(R4), ALU.add)
+    for b in range(4):
+        fill(["w1.z%d" % b], T.w1[:, W1 * b + NIL:W1 * (b + 1)], 0.0)
+    fill(["m0.z"], T.m0[:, 4 * C:], 0.0)
+    fill(["g1.z"], T.g1[:, 4 * C:], 0.0)
+    ts(["isl", "h4"], ["tc"], T.tc[:], T.isl[:], pf(H4), ALU.add, float(C), ALU.add)
+    for b in range(4):
+        move("S", ["h2.%d" % b], ["w2.l%d" % b], T.w2[:, W2 * b:W2 * b + C], T.h2[:, b:4 * C:4])
+
+    slots = lambda t: T.cw[:, CW * t + P0 + 1:CW * t + P0 + 1 + A]
 
     def ol_steps(t):
         return [
-            lambda: ts(["jb", "cn"], ["oa"], T.oa[:], T.jb[:, 1:A + 1], T.cn[:, 0:1], ALU.is_ge, float(C), ALU.mult),
-            lambda: tt(["oa", "cw%d" % t], ["ob"], T.ob[:], T.oa[:], T.cw[:, CW * t + C + 1:CW * t + C + 1 + A], ALU.add),
-            lambda: ts(["ob"], ["od"], T.od[:], T.ob[:], float(2 * C), ALU.is_ge, float(-2 * C - 1), ALU.mult),
+            lambda: ts(["jb", "cn"], ["oa"], T.oa[:], T.jb[:, 0:A], cn, ALU.is_ge, float(C), ALU.mult),
+            lambda: tt(["oa", "cw%d" % t], ["ob"], T.ob[:], T.oa[:], slots(t), ALU.add),
+            lambda: ts(["ob"], ["od"], T.od[:], T.ob[:], float(2 * C), ALU.is_ge, float(-NIL - C - 1), ALU.mult),
             lambda: tt(["ob", "od"], ["olb%d" % t], T.olb[:, A * t:A * t + A], T.ob[:], T.od[:], ALU.add),
         ]
 
-    def list_steps(k, limit, limit_key):
-        raw = T.e4[:, 7:2 * C:8]
-        sl = slice(48 * k, 48 * k + 48)
-        return [
-            lambda: ts(["e4", limit_key], ["la%d" % k], T.la[:, sl], raw, limit, ALU.is_gt, -BIG, ALU.mult),
-            lambda: tt(["e4", "la%d" % k], ["lb%d" % k], T.lb[:, sl], raw, T.la[:, sl], ALU.add),
-            lambda: tt(["lb%d" % k, "jh"], ["lc%d" % k], T.lc[:, sl], T.lb[:, sl], T.jh[:], ALU.max),
-            lambda: ts(["lc%d" % k, "ca"], ["lst%d" % k], T.lst[:, sl], T.lc[:, sl], 4.0, ALU.mult, pf(CA), ALU.add),
-        ]
+    raw = T.e16[:, 31:2 * C:32]
+
+    def list_steps(t):
+        first, last = t == 0, t == R - 1
+        sl = slice(12 if last else 0, 24)
+        now, key = (T.cur, "cur") if first else (T.lf, "lf")
+        half = lambda buf, k: buf[:, 12 * k:12 * k + 12]
+        steps = {
+            "cn": lambda: ts(["cum0"], ["cn"], cn, T.cum0[:, 0:1], -1.0, ALU.mult, float(P0 + 1), ALU.add),
+            "lim": lambda: ts(["cum0", "pf%d" % LA, "pf%d" % LB], ["lim"], T.lim[:, 0:1], T.cum0[:, 0:1], pf(LA), ALU.add, pf(LB), ALU.min),
+            "pos": lambda: ts(["e16", "cn", "pf%d" % HC], ["pos"], T.pos[:], raw, cn, ALU.add, pf(HC), ALU.subtract),
+            "la0": lambda: ts(["e16", "lim"], ["la0"], half(T.la, 0), raw, T.lim[:, 0:1], ALU.is_le),
+            "la1": lambda: ts(["e16", "cn", "pf%d" % LC], ["la1"], half(T.la, 1), raw, cn, ALU.add, pf(LC), ALU.is_le),
+            "lb0": lambda: tt(["pos", "la0"], ["lb0"], half(T.lb, 0), T.pos[:], half(T.la, 0), ALU.mult),
+            "lb1": lambda: tt(["pos", "la1"], ["lb1"], half(T.lb, 1), T.pos[:], half(T.la, 1), ALU.mult),
+            "lf": lambda: tt(["lb0", "lb1", "jc0", "jc1"], [key], now[:, sl], T.lb[:, sl], T.jc[:, sl], ALU.max),
+            "lg": lambda: ts(["lf"], ["lg"], T.lg[:, sl], T.lf[:, sl], float(C), ALU.is_ge, float(A * t), ALU.mult),
+            "lh": lambda: tt(["lf", "lg"], ["lh"], T.lh[:, sl], T.lf[:, sl], T.lg[:, sl], ALU.add),
+            "cur": lambda: tt(["lh", "cur"], ["cur"], T.cur[:, sl], T.lh[:, sl], T.cur[:, sl], ALU.max),
+            "ls": lambda: cp(["cur"], ["ls%d" % t], T.ls[:, LW * t + sl.start:LW * t + LW], T.cur[:, sl]),
+            "own": lambda: cp([key], ["lown"], T.lown[:], now[:, 0:12]),
+            "ta": lambda: ts(["isl", "cn"], ["ta"], T.ta[:], T.isl[:], cn, ALU.is_lt, BIG, ALU.mult),
+            "tb": lambda: tt(["ta", "tc"], ["tb"], T.tb[:], T.ta[:], T.tc[:], ALU.min),
+            "td": lambda: tt(["tb", "e2"], ["td"], T.td[:], T.tb[:], T.e2[:, 3:A:4], ALU.max),
+            "off1": lambda: ts(["td", "ca1"], ["off1"], T.off1[:], T.td[:], pf(CA1), ALU.add),
+        }
+        skip = (["lg", "lh", "cur"] if first else []) + (["lim", "la0", "lb0", "own"] if last else [])
+        return lambda *names: [steps[n]() for n in names if n not in skip]
 
     for t in range(R):
-        last = t == R - 1
-        wn, wo = ("w2a", "w2b") if t % 2 == 0 else ("w2b", "w2a")
-        W2, W2o = T[wn], T[wo]
-        a0, a1 = C * 2 * t, C * (2 * t + 1)
-        for b in range(4):
-            mm(["qe", "ql%d" % (2 * t)], b, T.qe, T.se, 128 * b, T.ql, T.sl, a0, C)
-        for b in range(4):
-            act(["ps%d" % b], ["g0.%d" % b], T.g0[:, b:4 * C:4], bank(b, C))
-        sums = [(lambda b=b: tt(["ps%d" % b, "h0"], ["m0.%d" % b], T.m0[:, b:4 * C:4], bank(b, C), T.h0[:, b:4 * C:4], ALU.add))
-                for b in range(4)]
-        sums[0]()
-        sums[1]()
+        first, last = t == 0, t == R - 1
+        new = C + A * (t - 1)
+        M = T["m%d" % t]
+
+        def add(b):
+            if first:
+                tt(["ps%d" % b, "h0"], ["m0.%d" % b], M[:, b:4 * C:4], bank(b, C), T.h0[:, b:4 * C:4], ALU.add)
+
+        def unpack(k):
+            a, n = piece(t, k)
+            for b in range(4):
+                mm(["qe%d" % b, "ql%d" % (2 * t + k)], 4 * k + b, T.qe, T.se, 128 * b, T.ql, T.sl, a, n)
+
+        def log(k):
+            G, win, name = T["g%d" % k], T["wg%d" % k], "g%d.%%d" % k
+            for b in range(4):
+                if first:
+                    move(PAIR[b], ["ps%d" % (4 * k + b)], [name % b], G[:, b:4 * C:4], bank(4 * k + b, C))
+                else:
+                    at = WG * b + new
+                    move(PAIR[b], ["ps%d" % (4 * k + b)], ["w" + name % b], win[:, at:at + A], bank(4 * k + b, A))
+            if not first:
+                came = T.rl[:, LW * (t - 1) + 12 * k:LW * (t - 1) + 12 * k + 12]
+                for b in range(4):
+                    move(PAIR[b], ["w" + name % b, "rl%d" % (t - 1)], [name % b], G[:, b:4 * C:4],
+                         win[:, WG * b:WG * b + new + A].indirect(came))
+
+        unpack(0)
+        log(0)
+        add(0)
         quant(four("g0"), ["qg0"], T.qg, T.sg, 0, C, T.g0[:])
+        add(1)
+        if not first:
+            dma("G", "d_add", four("g0"), four("m%d" % t), M[:, 0:4 * C], T.g0[:], accum_op=ALU.add)
+        if t == 1:
+            round_constants(2)
+        unpack(1)
         mm(["qup", "sup", "qg0"], 0, T.qup, T.sup, 0, T.qg, T.sg, 0, C)
-        sums[2]()
-        for b in range(4):
-            mm(["qe", "ql%d" % (2 * t + 1)], 4 + b, T.qe, T.se, 128 * b, T.ql, T.sl, a1, C)
+        log(1)
         tt(["ps0", "p0"], ["nl"], T.nl[:], bank(0, C), T.p0[:], ALU.is_le)
-        tt(["ps0", "p1"], ["top"], T.top[:], bank(0, C), T.p1[:], ALU.max)
-        ts(["nl"], ["nb"], T.nb[:], T.nl[:], -1e29, ALU.mult)
-        sums[3]()
-        for b in range(4):
-            act(["ps%d" % (4 + b)], ["g1.%d" % b], T.g1[:, b:4 * C:4], bank(4 + b, C))
         quant(four("g1"), ["qg1"], T.qg, T.sg, C, C, T.g1[:, 0:4 * C])
         mm(["qup", "sup", "qg1"], 1, T.qup, T.sup, 0, T.qg, T.sg, C, C)
+        ts(["nl"], ["nb"], T.nb[:], T.nl[:], -1e29, ALU.mult)
+        tt(["ps0", "p1"], ["top"], T.top[:], bank(0, C), T.p1[:], ALU.max)
         tt(["ps0", "nb"], ["thr"], T.thr[:], bank(0, C), T.nb[:], ALU.add)
-        if t == 0:
-            late_constants[0]()
-        l2 = list_steps(1, pf(C320), "c320")
-        l1 = ol_steps(t) if last else list_steps(0, T.cn[:, 1:2], "lim")
+        if first:
+            for k in range(2):
+                for b in range(4):
+                    move("S", ["g%d.%d" % (k, b)], ["wg%d.%d" % (k, b)], T["wg%d" % k][:, WG * b:WG * b + C], T["g%d" % k][:, b:4 * C:4])
+        else:
+            halves_of_h1()
+            for b in range(4):
+                at = W2 * b + new
+                move("S", ["t1.%d" % b], ["w2.l%d" % b], T.w2[:, at:at + A], T.t1[:, b:4 * A:4])
+        short, ol = list_steps(t), ol_steps(t)
+        down = slice(C - 1, None, -1)
         tt(["ps1", "top"], ["fl.1"], T.fl[:, C:2 * C], bank(1, C), T.top[:], ALU.is_gt)
         tt(["ps1", "thr"], ["fl.0"], T.fl[:, 0:C], bank(1, C), T.thr[:], ALU.is_le)
-        if t == 0:
-            late_constants[1]()
-            late_constants[2]()
-        scan(["fl.0", "fl.1", "step.0", "step.1", "step.2"], ["cum"], T.cum[:], T.fl[:], T.step[:], float(C + 1), ALU.add, ALU.subtract)
-        if t == 0:
-            late_constants[3]()
-            late_constants[4]()
-        scan(["cum", "fl.0"], ["xx.0"], T.xx[:, 0:2 * C:2], T.cum[:, 0:C], T.fl[:, 0:C], 0.0, ALU.max, ALU.mult)
-        scan(["cum", "fl.1"], ["xx.1"], T.xx[:, 1:2 * C:2], T.cum[:, C:2 * C], T.fl[:, C:2 * C], 0.0, ALU.max, ALU.mult)
-        cp(["cum"], ["cn"], T.cn[:, 0:1], T.cum[:, C - 1:C])
+        scan(["fl.1"], ["cum1"], T.cum1[:], T.fl[:, C:2 * C], T.fl[:, C:2 * C], float(P0), ALU.add, ALU.max)
+        scan(["fl.0", "one"], ["cum0"], T.cum0[:, down], T.one[:], T.fl[:, down], float(P0 + 1 - C), ALU.add, ALU.subtract)
+        scan(["cum1", "fl.1"], ["xx.1"], T.xx[:, 1:2 * C:2], T.cum1[:], T.fl[:, C:2 * C], 0.0, ALU.max, ALU.mult)
+        scan(["cum0", "fl.0"], ["xx.0"], T.xx[:, 0:2 * C:2], T.cum0[:], T.fl[:, 0:C], 0.0, ALU.max, ALU.mult)
+        short("cn", "lim")
         scan(["xx.0", "xx.1", "m16.e", "m16.o"], ["e16"], T.e16[:], T.m16[:], T.xx[:], 0.0, ALU.add, ALU.max)
-        scan(["xx.0", "xx.1", "m4.e", "m4.o"], ["e4"], T.e4[:], T.m4[:], T.xx[:], 0.0, ALU.add, ALU.max)
-        ts(["e16", "h16"], ["offs"], T.offs[:], T.e16[:, 31:2 * C:32], pf(H16), ALU.subtract)
-        if not last:
-            ts(["cn", "c191", "c320"], ["lim"], T.cn[:, 1:2], T.cn[:, 0:1], pf(C191), ALU.add, pf(C320), ALU.min)
-        ts(["isl", "cn"], ["ta"], T.ta[:], T.isl[:], T.cn[:, 0:1], ALU.is_lt, BIG, ALU.mult)
+        add(2)
+        short("ta")
+        ts(["e16", "cn", "h16"], ["offs"], T.offs[:], raw, cn, ALU.add, pf(H16), ALU.subtract)
+        add(3)
+        short("pos", "la0", "la1")
         cp(["offs", "jb"], ["cw%d" % t], T.cw[:, CW * t:CW * t + CW].indirect(T.offs[:, 0:12]), T.jb[:])
-        l1[0]()
-        tt(["ta", "tc"], ["tb"], T.tb[:], T.ta[:], T.tc[:], ALU.min)
-        scan(["cw%d" % t, "m4.e"], ["e2"], T.e2[:], T.m4[:, 0:2 * A:2], T.cw[:, CW * t + C + 1:CW * t + C + 1 + A], 0.0, ALU.add, ALU.max)
-        if last:
-            l2[0]()
-        else:
-            l1[1]()
-        ts(["e2", "ca"], ["off0"], T.off0[:], T.e2[:, 3:A:4], 4.0, ALU.mult, pf(CA), ALU.add)
-        tt(["tb", "e2"], ["td"], T.td[:], T.tb[:], T.e2[:, 3:A:4], ALU.max)
-        mw = four("m0") + ["m0.z", "off0"]
-        act(mw, ["z0.1"], T.z0[:, 256:512], T.m0[:].indirect(T.off0[:, 16:32]), scale=0.5)
-        ts(mw, ["z0.0"], T.z0[:, 0:256], T.m0[:].indirect(T.off0[:, 0:16]), 0.5, ALU.mult)
-        act(four("g1") + ["g1.z", "off0"], ["g1e"], T.g1e[:], T.g1[:].indirect(T.off0[:, 0:32]), scale=0.5)
-        ts(["td", "ca"], ["off1"], T.off1[:], T.td[:], 4.0, ALU.mult, pf(CA), ALU.add)
-        (l2[1] if last else l1[2])()
+        short("lb0", "lb1")
+        scan(["cw%d" % t, "m4"], ["e2"], T.e2[:], T.m4[:], slots(t), 0.0, ALU.add, ALU.max)
+        short("tb", "lf")
+        ts(["e2", "ca0"], ["off0"], T.off0[:], T.e2[:, 3:A:4], 4.0, ALU.mult, pf(CA0), ALU.add)
+        short("td", "lg")
+        mw, gw, cut = four("m%d" % t) + ["m%d.z" % t, "off0"], four("g1") + ["g1.z", "off0"], 20
+        move("S", mw, ["z0.1"], T.z0[:, 256:512], M[:].indirect(T.off0[:, 16:32]), 0.5)
+        move("V", mw, ["z0.0"], T.z0[:, 0:256], M[:].indirect(T.off0[:, 0:16]), 0.5)
+        move("S", gw, ["g1e.0"], T.g1e[:, 0:16 * cut], T.g1[:].indirect(T.off0[:, 0:cut]), 0.5)
+        short("off1", "lh")
         quant(["z0.0", "z0.1"], ["qz0"], T.qz, T.sz, 0, A, T.z0[:])
         for a in range(4):
             mm(["qw", "sw", "qz0"], 4 + a, T.qw, T.sw, 128 * a, T.qz, T.sz, 0, A)
-        if last:
-            l1[1]()
-            l2[2]()
-        else:
-            l1[3]()
-            l2[0]()
-        for a in range(3):
-            ts(["ps%d" % (4 + a)], ["w1h.t%d" % a], T.w1h[:, TB + a:TB + 4 * A:4], bank(4 + a, A), 0.0, ALU.max, 2.0 ** -6, ALU.mult)
-        act(["ps7"], ["w1h.t3"], T.w1h[:, TB + 3:TB + 4 * A:4], bank(7, A), ACT.Relu, 2.0 ** -6)
-        (l1[2] if last else l2[1])()
-        w1 = ["w1h.l", "w1h.z"] + ["w1h.t%d" % a for a in range(4)]
-        tt(w1 + ["off1", "g1e"], ["z1"], T.z1[:], T.w1h[:, 0:TB + 4 * A].indirect(T.off1[:, 0:32]), T.g1e[:], ALU.add)
+        short("cur")
+        move("V", gw, ["g1e.1"], T.g1e[:, 16 * cut:], T.g1[:].indirect(T.off0[:, cut:32]), 0.5)
+        short("own")
+        for a in range(4):
+            relu(PAIR[a] if last else "SVVV"[a], ["ps%d" % (4 + a)], ["w1.t%d" % a], T.w1[:, W1 * a + C:W1 * a + NIL], bank(4 + a, A), 2.0 ** -6)
+        short("ls")
+        ol[0]()
         if not last:
-            act(w1 + ["lst0"], ["h1"], T.h1[:], T.w1h[:, 0:TB + 4 * A].indirect(T.lst[:, 0:48]), scale=2.0)
-        (l2[3] if last else l2[2])()
+            remote("ls%d" % t, "arl%d" % t, "sent", "rl%d" % t, [(T.rl[:, LW * t:LW * t + LW], T.ls[:, LW * t:LW * t + LW])])
+            for a in range(4):
+                move("S", ["w1.t%d" % a], ["t0.%d" % a], T.t0[:, a:4 * A:4], T.w1[:, W1 * a + C:W1 * a + NIL], 2.0)
+        plane1 = lambda b: ["w1.l%d" % b, "w1.z%d" % b, "w1.t%d" % b]
+        merge1 = lambda q, b: move(q, plane1(b) + ["lown"], ["h1.%d" % b], T.h1[:, b:4 * C:4],
+                                   T.w1[:, W1 * b:W1 * b + NIL].indirect(T.lown[:]), 2.0)
+        tt(sum([plane1(b) for b in range(4)], []) + ["off1", "g1e.0", "g1e.1"], ["z1"], T.z1[:], T.w1[:].indirect(T.off1[:, 0:32]), T.g1e[:], ALU.add)
+        if last:
+            ol[1]()
+        else:
+            quant(four("t0"), ["qh%d" % (2 * t + 2)], T.qh, T.sh, piece(t + 1, 0)[0], A, T.t0[:])
+            send(t + 1, 0)
+            merge1("S", 0)
+            merge1("S", 1)
         quant(["z1"], ["qz1"], T.qz, T.sz, A, A, T.z1[:])
         for a in range(4):
             mm(["qw", "sw", "qz1"], 4 + a, T.qw, T.sw, 128 * a, T.qz, T.sz, A, A)
         if not last:
-            l2[3]()
-            quant(["h1"], ["qh%d" % (2 * t + 2)], T.qh, T.sh, a0 + 2 * C, C, T.h1[:])
-            send(t + 1, 0)
-            mm(["qup", "sup", "qh%d" % (2 * t + 2)], 2, T.qup, T.sup, 0, T.qh, T.sh, a0 + 2 * C, C)
-        else:
-            l1[3]()
-            dma("Y", "d_out", ["olb0", "olb1", "olb2"], [], T.ol[:], T.olb[0:128:16, :])
-        for a in ((0, 2) if last else (0, 1)):
-            act(["ps%d" % (4 + a)], ["%s.t%d" % (wn, a)], W2[:, TB + a:TB + 4 * A:4], bank(4 + a, A), ACT.Relu, 2.0 ** -5)
-        for a in ((1, 3) if last else (2, 3)):
-            ts(["ps%d" % (4 + a)], ["%s.t%d" % (wn, a)], W2[:, TB + a:TB + 4 * A:4], bank(4 + a, A), 0.0, ALU.max, 2.0 ** -5, ALU.mult)
-        w2 = [wn + ".l0", wn + ".l1", wn + ".z", "lst1"] + ["%s.t%d" % (wn, a) for a in range(4)]
-        act(w2, [wo + ".l1"], W2o[:, 2 * C:4 * C], W2[:, 0:TB + 4 * A].indirect(T.lst[:, 72:96]))
-        cp(w2, [wo + ".l0"], W2o[:, 0:2 * C], W2[:, 0:TB + 4 * A].indirect(T.lst[:, 48:72]))
-        if not last:
-            quant([wo + ".l0", wo + ".l1"], ["qh%d" % (2 * t + 3)], T.qh, T.sh, a1 + 2 * C, C, W2o[:, 0:4 * C])
+            merge1("V", 2)
+            for a in range(4):
+                relu(PAIR[a], ["ps%d" % (4 + a)], ["t1.%d" % a], T.t1[:, a:4 * A:4], bank(4 + a, A), 2.0 ** -5)
+            merge1("S", 3)
+            quant(four("t1"), ["qh%d" % (2 * t + 3)], T.qh, T.sh, piece(t + 1, 1)[0], A, T.t1[:])
             send(t + 1, 1)
-            act(["ps2"], ["p1"], T.p1[:], bank(2, C))
-            act(["h1"], ["w1h.l"], T.w1h[:, 0:4 * C], T.h1[:], scale=0.5)
-            steps = ol_steps(t)
-            steps[0]()
-            if t == 0:
+            ol[1]()
+            quant(four("h1"), ["q1"], T.q1, T.s1, 0, C, T.h1[:])
+            mm(["qup", "sup", "q1"], 4, T.qup, T.sup, 0, T.q1, T.s1, 0, C)
+            act(["ps4"], ["p1"], T.p1[:], bank(4, C))
+            ol[2]()
+            if first:
                 quant(["vt"], ["qv"], T.qv, T.sv, 0, 128, T.vt[:])
-            for step in steps[1:]:
-                step()
+            ol[3]()
         else:
-            quant([wo + ".l0", wo + ".l1"], ["qf"], T.qf, T.sf, 0, C, W2o[:, 0:4 * C])
+            ol[2]()
+            ol[3]()
+            dma("Y", "d_out", ["olb0", "olb1", "olb2"], [], T.ol[:], T.olb[0:128:16, :])
+            for a in range(4):
+                relu(PAIR[a], ["ps%d" % (4 + a)], ["w2.t%d" % a], T.w2[:, W2 * a + C + A * t:W2 * (a + 1)], bank(4 + a, A), 2.0 ** -5)
+            for b in range(4):
+                move(PAIR[b], ["w2.l%d" % b, "w2.t%d" % b, "ls%d" % t], ["h2.%d" % b], T.h2[:, b:4 * C:4],
+                     T.w2[:, W2 * b:W2 * (b + 1)].indirect(T.ls[:, LW * t + 12:LW * t + LW]))
+            quant(four("h2"), ["qf"], T.qf, T.sf, 0, C, T.h2[:])
             mm(["qv", "qf"], 0, T.qv, T.sv, 0, T.qf, T.sf, 0, C)
             dma("Y", "d_out", ["qf"], [], T.oc[:], T.qf[:].bitcast(dt.uint8))
             for k in range(4):

from concourse.mybir import dt, AluOpType, ActivationFunctionType

ALU, ACT = AluOpType, ActivationFunctionType
C, A, R, N = 192, 128, 3, 8
F16, BF, F32, I32, U16, U8 = "float16", "bfloat16", "float32", "int32", "uint16", "uint8"
BIG = 4096.0
HOLD, LIFT = 512.0, 1024.0
NIL = C + A
W1 = NIL + 16
W2 = C + R * A
WG = C + (R - 1) * A
P0 = 2 * C - 1
CW = P0 + 1 + C
SENT = 2 * C + 2 * (R - 1) * A
LW = 24
QX = "float8_e4m3fn_x4"

SCRATCH = {"pa": ("psum", [128, 2048], F32), "pb": ("psum", [128, 2048], F32)}
for _dtype, _bufs in (
        (BF, dict(h0=4 * C, h1=4 * C, h2=4 * C, w1=4 * W1, w2=4 * W2, wg0=4 * WG, wg1=4 * WG, m0=4 * NIL + 16,
                  m1=4 * NIL + 16, m2=4 * NIL + 16, g0=4 * C, g1=4 * NIL + 16, g1e=4 * A, z0=4 * A, z1=4 * A, t0=4 * A,
                  t1=4 * A, ut=512, vt=512, et=520, jb=C, jm=C + 16, jr=A, one=C, nl=C, nb=C, cw=R * CW, oa=A, ka=C,
                  kb=C + 2, m16=2 * C, m4a=A, m4=A)),
        (QX, dict(qe=512, qw=512, qu=128, qup=128, qv=128, q0=C, q1=C, qh=SENT, ql=SENT, qg=2 * C, qz=2 * A, qf=C)),
        (U8, dict(se=512, sw=512, su=128, sup=128, sv=128, s0=C, s1=C, sh=SENT, sl=SENT, sg=2 * C, sz=2 * A, sf=C)),
        (F16, dict(fl=2 * C, cum0=C, cum1=C, xx=2 * C, e16=2 * C, e2=A, ob=A, od=A)),
        (F32, dict(dmat=128, pf=16, c4=48, jc=24, pos=12, cn=2, tc=32, isl=32, p0=C, p1=C, top=C, thr=C, lim=2, ta=32,
                   tb=32, td=32, la=24, lb=24, lf=24, lg=24, lh=24, cur=24, olb=R * A, yb=C)),
        (I32, dict(pint=8)),
        (U16, dict(offu=8, offs=12, off0=32, off1=32, lown=12, ls=LW * R, rl=LW * (R - 1)))):
    for _name, _cols in _bufs.items():
        SCRATCH[_name] = ("sbuf", [128, _cols], _dtype)
DMAS = ["d_h1", "d_h2", "d_u", "d_h0", "d_wc", "d_ws", "d_v", "d_m1", "d_m2", "d_add", "d_out"]
SEMAPHORES = (["cv", "cs", "cp", "cg", "sent0", "sent"] + ["arr%d" % i for i in range(2 * R)]
              + ["arl%d" % i for i in range(R - 1)] + DMAS)


def rank_program(g, core, T, topo):
    rank = T.rank_of(core)
    if rank is None:
        return
    nxt = T.cores[(rank + 1) % N]
    rid, pid = topo.addr(nxt, core)
    mask = topo.mask(core, nxt)
    engines = len(topo.engines(core, nxt))

    queue = {"V": g.vector, "S": g.scalar, "P": g.tensor, "G": g, "Y": g.sync}
    own = {"V": "cv", "S": "cs", "P": "cp", "G": "cg"}
    count = {}
    clock = {q: {} for q in queue}
    writer, readers = {}, {}

    def need(q, ev):
        sem, n, seen = ev
        if clock[q].get(sem, 0) >= n:
            return
        queue[q].wait_ge(T.sem[sem], n)
        for s, m in seen.items():
            if clock[q].get(s, 0) < m:
                clock[q][s] = m
        clock[q][sem] = n

    def order(q, r, w):
        evs = []
        for k in r:
            if k in writer:
                evs.append(writer[k])
            if k.startswith("ps"):
                evs += [e for (qq, e) in readers.get(k, []) if qq != q]
        for k in w:
            if k in writer:
                evs.append(writer[k])
            evs += [e for (qq, e) in readers.get(k, [])]
        best = {}
        for e in evs:
            if e[0] not in best or best[e[0]][1] < e[1]:
                best[e[0]] = e
        for e in sorted(best.values(), key=lambda e: -sum(e[2].values())):
            need(q, e)

    def note(q, ev, r, w):
        for k in r:
            readers.setdefault(k, []).append((q, ev))
        for k in w:
            writer[k] = ev
            readers[k] = []

    def op(q, r, w, call):
        order(q, r, w)
        sem = own[q]
        count[sem] = count.get(sem, 0) + 1
        call().then_inc(T.sem[sem], 1)
        note(q, (sem, count[sem], dict(clock[q])), r, w)

    def dma(q, sem, r, w, out, in_, **how):
        order(q, r, w)
        count[sem] = count.get(sem, 0) + 16
        queue[q].dma_start(out, in_, **how).then_inc(T.sem[sem], 16)
        note(q, (sem, count[sem], dict(clock[q])), r, w)

    V, S, P = g.vector, g.scalar, g.tensor

    def ts(r, w, out, in0, s1, op0, s2=None, op1=None):
        if op1 is None:
            op("V", r, w, lambda: V.tensor_scalar(out, in0, s1, None, op0))
        else:
            op("V", r, w, lambda: V.tensor_scalar(out, in0, s1, s2, op0, op1))

    def tt(r, w, out, in0, in1, o):
        op("V", r, w, lambda: V.tensor_tensor(out, in0, in1, o))

    def scan(r, w, out, d0, d1, init, op0, op1):
        op("V", r, w, lambda: V.tensor_tensor_scan(out, d0, d1, init, op0, op1))

    def cp(r, w, out, in_):
        op("V", r, w, lambda: V.tensor_copy(out, in_))

    def fill(w, ap, c):
        op("V", [], w, lambda: V.memset(ap, c))

    def act(r, w, out, in_, func=ACT.Copy, scale=1.0):
        if scale == 1.0:
            op("S", r, w, lambda: S.activation(out, in_, func))
        else:
            op("S", r, w, lambda: S.activation(out, in_, func, scale=scale))

    def move(q, r, w, out, in_, scale=1.0):
        if q == "S":
            act(r, w, out, in_, scale=scale)
        elif scale == 1.0:
            cp(r, w, out, in_)
        else:
            ts(r, w, out, in_, scale, ALU.mult)

    def relu(q, r, w, out, in_, scale):
        if q == "S":
            act(r, w, out, in_, ACT.Relu, scale)
        else:
            ts(r, w, out, in_, 0.0, ALU.max, scale, ALU.mult)

    def iota(w, out, pattern, base, per_partition, whole=False):
        if whole:
            op("G", [], w, lambda: g.iota(out, pattern, base, per_partition))
        else:
            op("G", [], w, lambda: g.iota(out, pattern, base, per_partition, allow_small_or_imprecise_dtypes=True))

    def quant(r, w, q, s, a, n, tile):
        op("V", r, w, lambda: V.quantize_mx(q[:, a:a + n], s[:, a:a + n], tile))

    def bank(i, n):
        buf = T.pa if i < 4 else T.pb
        return buf[:, 512 * (i % 4):512 * (i % 4) + n]

    def mm(r, i, lq, ls, la, rq, rs, ra, n):
        op("P", r, ["ps%d" % i], lambda: P.matmul_mx(bank(i, n), lq[:, la:la + 128], ls[:, la:la + 128],
                                                    rq[:, ra:ra + n], rs[:, ra:ra + n], True, True))

    def piece(t, k):
        return (C * k, C) if t == 0 else (2 * C + A * (2 * t - 2 + k), A)

    def remote(key, arr, loc, lands, pairs):
        order("G", [key], [])
        for out, in_ in pairs:
            g.remote_dma(out, in_, T.sem[arr], T.sem[loc], pid, rid, mask)
        count[loc] = count.get(loc, 0) + len(pairs) * engines
        count[arr] = len(pairs) * engines
        writer[lands] = (arr, count[arr], {})

    def send(t, k):
        i = 2 * t + k
        a, n = piece(t, k)
        remote("qh%d" % i, "arr%d" % i, "sent0" if t == 0 else "sent", "ql%d" % i,
               [(T.ql[:, a:a + n].bitcast(dt.uint8), T.qh[:, a:a + n].bitcast(dt.uint8)), (T.sl[:, a:a + n], T.sh[:, a:a + n])])

    four = lambda name: ["%s.%d" % (name, b) for b in range(4)]
    pf = lambda i: T.pf[:, i:i + 1]
    Q16, T4, R4, H16, H4, CA0, CA1, LA, LB, LC, HC = range(11)
    cn = T.cn[:, 0:1]
    PAIR = "SVSV"

    dma("Y", "d_h1", [], four("h1"), T.h1[:], T.x[:, 4 * C:8 * C])
    dma("Y", "d_h2", [], four("h2"), T.h2[:], T.x[:, 8 * C:12 * C])
    dma("Y", "d_u", [], ["ut"], T.ut[:], T.u[:])
    dma("Y", "d_h0", [], ["h0"], T.h0[:], T.x[:, 0:4 * C])

    iota(["dmat"], T.dmat[:], [[1, 128]], 0, -1)
    iota(["pi"], T.pint[:, 0:1], [[1, 1]], 0, 1, True)
    iota(["c4"], T.c4[:], [[4, 48]], 0, 0)
    iota(["jm"], T.jm[:], [[0, 13], [1, 16]], 0, 0)
    iota(["jb"], T.jb[:], [[1, C]], 0, 0)
    fill(["et"], T.et[:], 0.0)
    fill(["one"], T.one[:], 1.0)
    ts(["dmat"], ["et"], T.et[:, 3:515:4], T.dmat[:], 0.0, ALU.is_equal)
    ts(["pi"], ["pi1"], T.pint[:, 1:2], T.pint[:, 0:1], 15, ALU.bitwise_and)
    ts(["pi"], ["pi2"], T.pint[:, 2:3], T.pint[:, 0:1], 3, ALU.bitwise_and)
    ts(["pi"], ["pi3"], T.pint[:, 3:4], T.pint[:, 0:1], 2, ALU.logical_shift_right, 3, ALU.bitwise_and)
    for b in range(4):
        quant(["et"], ["qe%d" % b], T.qe, T.se, 128 * b, 128, T.et[:, 3 - b:515 - b])
        if b == 0:
            cp(["pi1", "pi2", "pi3"], ["pf"], T.pf[:, 0:3], T.pint[:, 1:4])
    ts(["c4"], ["offu"], T.offu[:], T.c4[:, 0:8], 4.0, ALU.mult)
    ts(["pf"], ["h4"], pf(H4), pf(R4), -HOLD, ALU.mult, 3 * HOLD, ALU.add)
    ts(["pf"], ["h16"], pf(H16), pf(Q16), 15.0, ALU.is_lt, LIFT, ALU.mult)

    def halves_of_h1():
        for b in range(4):
            move("S", ["h1.%d" % b], ["w1.l%d" % b], T.w1[:, W1 * b:W1 * b + C], T.h1[:, b:4 * C:4], 0.5)

    def round_constants(t):
        iota(["cw%d" % t], T.cw[:, CW * t:CW * t + CW], [[0, CW]], NIL, 0)
        if t > 0:
            iota(["m%d.z" % t], T["m%d" % t][:, 4 * C:], [[0, 4 * A + 16]], 0, 0)

    quant(four("h1"), ["qh0"], T.qh, T.sh, 0, C, T.h1[:])
    send(0, 0)
    ts(["jm", "pf"], ["kb"], T.kb[:, 0:C + 1], T.jm[:, 15:C + 16], pf(Q16), ALU.is_equal, LIFT, ALU.mult)
    halves_of_h1()
    quant(four("h2"), ["qh1"], T.qh, T.sh, C, C, T.h2[:])
    send(0, 1)
    iota(["jr"], T.jr[:], [[0, A // 4], [1, 4]], 0, 0)
    round_constants(0)
    round_constants(1)
    need("Y", ("sent0", count["sent0"], {}))
    dma("Y", "d_wc", [], ["qw"], T.qw[:].bitcast(dt.uint8), T.wc[:])
    dma("Y", "d_ws", [], ["sw"], T.sw[:], T.ws[:])
    for t in range(1, R):
        dma("Y", "d_m%d" % t, [], four("m%d" % t), T["m%d" % t][:, 0:4 * C], T.x[:, 0:4 * C])
    dma("G", "d_v", ["qw", "sw"], ["vt"], T.vt[:], T.v[:])

    quant(["ut"], ["qu"], T.qu, T.su, 0, 128, T.ut[:])
    act(["kb"], ["ka"], T.ka[:], T.kb[:, 1:C + 1], scale=-2.0)
    tt(["kb", "jb"], ["m16.o"], T.m16[:, 1:2 * C:2], T.kb[:, 1:C + 1], T.jb[:], ALU.min)
    act(["qu", "offu"], ["sup"], T.sup[:, 0:128], T.su[:, 0:128].indirect(T.offu[:, 0:8]))
    cp(["qu", "offu"], ["qup"], T.qup[:, 0:128].bitcast(dt.uint32), T.qu[:, 0:128].bitcast(dt.uint32).indirect(T.offu[:, 0:8]))
    quant(["h0"], ["q0"], T.q0, T.s0, 0, C, T.h0[:])
    mm(["qup", "sup", "qh0"], 4, T.qup, T.sup, 0, T.qh, T.sh, 0, C)
    mm(["qup", "sup", "q0"], 5, T.qup, T.sup, 0, T.q0, T.s0, 0, C)
    act(["ps4"], ["p1"], T.p1[:], bank(4, C))
    act(["ps5"], ["p0"], T.p0[:], bank(5, C))
    tt(["ka", "kb"], ["m16.e"], T.m16[:, 0:2 * C:2], T.ka[:], T.kb[:, 0:C], ALU.add)
    ts(["jr", "pf"], ["m4a"], T.m4a[:], T.jr[:], pf(R4), ALU.is_equal, -BIG - HOLD, ALU.mult)
    ts(["h4", "pf"], ["ca0"], pf(CA0), pf(H4), -4.0, ALU.mult, pf(T4), ALU.add)
    ts(["h4", "pf"], ["ca1"], pf(CA1), pf(T4), float(W1), ALU.mult, pf(H4), ALU.subtract)
    for i, c in ((LA, A - 1), (LB, P0), (LC, P0 + A), (HC, C)):
        ts(["h16"], ["pf%d" % i], pf(i), pf(H16), float(c), ALU.add)
    ts(["m4a"], ["m4"], T.m4[:], T.m4a[:], HOLD, ALU.add)
    for k in range(2):
        ts(["c4", "pf"], ["jc%d" % k], T.jc[:, 12 * k:12 * k + 12], T.c4[:, 0:48:4], pf(Q16), ALU.add)
    ts(["c4", "pf"], ["isl"], T.isl[:], T.c4[:, 0:32], pf(R4), ALU.add)
    for b in range(4):
        fill(["w1.z%d" % b], T.w1[:, W1 * b + NIL:W1 * (b + 1)], 0.0)
    fill(["m0.z"], T.m0[:, 4 * C:], 0.0)
    fill(["g1.z"], T.g1[:, 4 * C:], 0.0)
    ts(["isl", "h4"], ["tc"], T.tc[:], T.isl[:], pf(H4), ALU.add, float(C), ALU.add)
    for b in range(4):
        move("S", ["h2.%d" % b], ["w2.l%d" % b], T.w2[:, W2 * b:W2 * b + C], T.h2[:, b:4 * C:4])

    slots = lambda t: T.cw[:, CW * t + P0 + 1:CW * t + P0 + 1 + A]

    def ol_steps(t):
        return [
            lambda: ts(["jb", "cn"], ["oa"], T.oa[:], T.jb[:, 0:A], cn, ALU.is_ge, float(C), ALU.mult),
            lambda: tt(["oa", "cw%d" % t], ["ob"], T.ob[:], T.oa[:], slots(t), ALU.add),
            lambda: ts(["ob"], ["od"], T.od[:], T.ob[:], float(2 * C), ALU.is_ge, float(-NIL - C - 1), ALU.mult),
            lambda: tt(["ob", "od"], ["olb%d" % t], T.olb[:, A * t:A * t + A], T.ob[:], T.od[:], ALU.add),
        ]

    raw = T.e16[:, 31:2 * C:32]

    def list_steps(t):
        first, last = t == 0, t == R - 1
        sl = slice(12 if last else 0, 24)
        now, key = (T.cur, "cur") if first else (T.lf, "lf")
        half = lambda buf, k: buf[:, 12 * k:12 * k + 12]
        steps = {
            "cn": lambda: ts(["cum0"], ["cn"], cn, T.cum0[:, 0:1], -1.0, ALU.mult, float(P0 + 1), ALU.add),
            "lim": lambda: ts(["cum0", "pf%d" % LA, "pf%d" % LB], ["lim"], T.lim[:, 0:1], T.cum0[:, 0:1], pf(LA), ALU.add, pf(LB), ALU.min),
            "pos": lambda: ts(["e16", "cn", "pf%d" % HC], ["pos"], T.pos[:], raw, cn, ALU.add, pf(HC), ALU.subtract),
            "la0": lambda: ts(["e16", "lim"], ["la0"], half(T.la, 0), raw, T.lim[:, 0:1], ALU.is_le),
            "la1": lambda: ts(["e16", "cn", "pf%d" % LC], ["la1"], half(T.la, 1), raw, cn, ALU.add, pf(LC), ALU.is_le),
            "lb0": lambda: tt(["pos", "la0"], ["lb0"], half(T.lb, 0), T.pos[:], half(T.la, 0), ALU.mult),
            "lb1": lambda: tt(["pos", "la1"], ["lb1"], half(T.lb, 1), T.pos[:], half(T.la, 1), ALU.mult),
            "lf": lambda: tt(["lb0", "lb1", "jc0", "jc1"], [key], now[:, sl], T.lb[:, sl], T.jc[:, sl], ALU.max),
            "lg": lambda: ts(["lf"], ["lg"], T.lg[:, sl], T.lf[:, sl], float(C), ALU.is_ge, float(A * t), ALU.mult),
            "lh": lambda: tt(["lf", "lg"], ["lh"], T.lh[:, sl], T.lf[:, sl], T.lg[:, sl], ALU.add),
            "cur": lambda: tt(["lh", "cur"], ["cur"], T.cur[:, sl], T.lh[:, sl], T.cur[:, sl], ALU.max),
            "ls": lambda: cp(["cur"], ["ls%d" % t], T.ls[:, LW * t + sl.start:LW * t + LW], T.cur[:, sl]),
            "own": lambda: cp([key], ["lown"], T.lown[:], now[:, 0:12]),
            "ta": lambda: ts(["isl", "cn"], ["ta"], T.ta[:], T.isl[:], cn, ALU.is_lt, BIG, ALU.mult),
            "tb": lambda: tt(["ta", "tc"], ["tb"], T.tb[:], T.ta[:], T.tc[:], ALU.min),
            "td": lambda: tt(["tb", "e2"], ["td"], T.td[:], T.tb[:], T.e2[:, 3:A:4], ALU.max),
            "off1": lambda: ts(["td", "ca1"], ["off1"], T.off1[:], T.td[:], pf(CA1), ALU.add),
        }
        skip = (["lg", "lh", "cur"] if first else []) + (["lim", "la0", "lb0", "own"] if last else [])
        return lambda *names: [steps[n]() for n in names if n not in skip]

    for t in range(R):
        first, last = t == 0, t == R - 1
        new = C + A * (t - 1)
        M = T["m%d" % t]

        def add(b):
            if first:
                tt(["ps%d" % b, "h0"], ["m0.%d" % b], M[:, b:4 * C:4], bank(b, C), T.h0[:, b:4 * C:4], ALU.add)

        def unpack(k):
            a, n = piece(t, k)
            for b in range(4):
                mm(["qe%d" % b, "ql%d" % (2 * t + k)], 4 * k + b, T.qe, T.se, 128 * b, T.ql, T.sl, a, n)

        def log(k):
            G, win, name = T["g%d" % k], T["wg%d" % k], "g%d.%%d" % k
            for b in range(4):
                if first:
                    move(PAIR[b], ["ps%d" % (4 * k + b)], [name % b], G[:, b:4 * C:4], bank(4 * k + b, C))
                else:
                    at = WG * b + new
                    move(PAIR[b], ["ps%d" % (4 * k + b)], ["w" + name % b], win[:, at:at + A], bank(4 * k + b, A))
            if not first:
                came = T.rl[:, LW * (t - 1) + 12 * k:LW * (t - 1) + 12 * k + 12]
                for b in range(4):
                    move(PAIR[b], ["w" + name % b, "rl%d" % (t - 1)], [name % b], G[:, b:4 * C:4],
                         win[:, WG * b:WG * b + new + A].indirect(came))

        unpack(0)
        log(0)
        add(0)
        quant(four("g0"), ["qg0"], T.qg, T.sg, 0, C, T.g0[:])
        add(1)
        if not first:
            dma("G", "d_add", four("g0"), four("m%d" % t), M[:, 0:4 * C], T.g0[:], accum_op=ALU.add)
        if t == 1:
            round_constants(2)
        unpack(1)
        mm(["qup", "sup", "qg0"], 0, T.qup, T.sup, 0, T.qg, T.sg, 0, C)
        log(1)
        tt(["ps0", "p0"], ["nl"], T.nl[:], bank(0, C), T.p0[:], ALU.is_le)
        quant(four("g1"), ["qg1"], T.qg, T.sg, C, C, T.g1[:, 0:4 * C])
        mm(["qup", "sup", "qg1"], 1, T.qup, T.sup, 0, T.qg, T.sg, C, C)
        ts(["nl"], ["nb"], T.nb[:], T.nl[:], -1e29, ALU.mult)
        tt(["ps0", "p1"], ["top"], T.top[:], bank(0, C), T.p1[:], ALU.max)
        tt(["ps0", "nb"], ["thr"], T.thr[:], bank(0, C), T.nb[:], ALU.add)
        if first:
            for k in range(2):
                for b in range(4):
                    move("S", ["g%d.%d" % (k, b)], ["wg%d.%d" % (k, b)], T["wg%d" % k][:, WG * b:WG * b + C], T["g%d" % k][:, b:4 * C:4])
        else:
            halves_of_h1()
            for b in range(4):
                at = W2 * b + new
                move("S", ["t1.%d" % b], ["w2.l%d" % b], T.w2[:, at:at + A], T.t1[:, b:4 * A:4])
        short, ol = list_steps(t), ol_steps(t)
        down = slice(C - 1, None, -1)
        tt(["ps1", "top"], ["fl.1"], T.fl[:, C:2 * C], bank(1, C), T.top[:], ALU.is_gt)
        tt(["ps1", "thr"], ["fl.0"], T.fl[:, 0:C], bank(1, C), T.thr[:], ALU.is_le)
        scan(["fl.1"], ["cum1"], T.cum1[:], T.fl[:, C:2 * C], T.fl[:, C:2 * C], float(P0), ALU.add, ALU.max)
        scan(["fl.0", "one"], ["cum0"], T.cum0[:, down], T.one[:], T.fl[:, down], float(P0 + 1 - C), ALU.add, ALU.subtract)
        scan(["cum1", "fl.1"], ["xx.1"], T.xx[:, 1:2 * C:2], T.cum1[:], T.fl[:, C:2 * C], 0.0, ALU.max, ALU.mult)
        scan(["cum0", "fl.0"], ["xx.0"], T.xx[:, 0:2 * C:2], T.cum0[:], T.fl[:, 0:C], 0.0, ALU.max, ALU.mult)
        short("cn", "lim")
        scan(["xx.0", "xx.1", "m16.e", "m16.o"], ["e16"], T.e16[:], T.m16[:], T.xx[:], 0.0, ALU.add, ALU.max)
        add(2)
        short("ta")
        ts(["e16", "cn", "h16"], ["offs"], T.offs[:], raw, cn, ALU.add, pf(H16), ALU.subtract)
        add(3)
        short("pos", "la0", "la1")
        cp(["offs", "jb"], ["cw%d" % t], T.cw[:, CW * t:CW * t + CW].indirect(T.offs[:, 0:12]), T.jb[:])
        short("lb0", "lb1")
        scan(["cw%d" % t, "m4"], ["e2"], T.e2[:], T.m4[:], slots(t), 0.0, ALU.add, ALU.max)
        short("tb", "lf")
        ts(["e2", "ca0"], ["off0"], T.off0[:], T.e2[:, 3:A:4], 4.0, ALU.mult, pf(CA0), ALU.add)
        short("td", "lg")
        mw, gw, cut = four("m%d" % t) + ["m%d.z" % t, "off0"], four("g1") + ["g1.z", "off0"], 20
        move("S", mw, ["z0.1"], T.z0[:, 256:512], M[:].indirect(T.off0[:, 16:32]), 0.5)
        move("V", mw, ["z0.0"], T.z0[:, 0:256], M[:].indirect(T.off0[:, 0:16]), 0.5)
        move("S", gw, ["g1e.0"], T.g1e[:, 0:16 * cut], T.g1[:].indirect(T.off0[:, 0:cut]), 0.5)
        short("off1", "lh")
        quant(["z0.0", "z0.1"], ["qz0"], T.qz, T.sz, 0, A, T.z0[:])
        for a in range(4):
            mm(["qw", "sw", "qz0"], 4 + a, T.qw, T.sw, 128 * a, T.qz, T.sz, 0, A)
        short("cur")
        move("V", gw, ["g1e.1"], T.g1e[:, 16 * cut:], T.g1[:].indirect(T.off0[:, cut:32]), 0.5)
        short("own")
        for a in range(4):
            relu(PAIR[a] if last else "SVVV"[a], ["ps%d" % (4 + a)], ["w1.t%d" % a], T.w1[:, W1 * a + C:W1 * a + NIL], bank(4 + a, A), 2.0 ** -6)
        short("ls")
        ol[0]()
        if not last:
            remote("ls%d" % t, "arl%d" % t, "sent", "rl%d" % t, [(T.rl[:, LW * t:LW * t + LW], T.ls[:, LW * t:LW * t + LW])])
            for a in range(4):
                move("S", ["w1.t%d" % a], ["t0.%d" % a], T.t0[:, a:4 * A:4], T.w1[:, W1 * a + C:W1 * a + NIL], 2.0)
        plane1 = lambda b: ["w1.l%d" % b, "w1.z%d" % b, "w1.t%d" % b]
        merge1 = lambda q, b: move(q, plane1(b) + ["lown"], ["h1.%d" % b], T.h1[:, b:4 * C:4],
                                   T.w1[:, W1 * b:W1 * b + NIL].indirect(T.lown[:]), 2.0)
        tt(sum([plane1(b) for b in range(4)], []) + ["off1", "g1e.0", "g1e.1"], ["z1"], T.z1[:], T.w1[:].indirect(T.off1[:, 0:32]), T.g1e[:], ALU.add)
        if last:
            ol[1]()
        else:
            quant(four("t0"), ["qh%d" % (2 * t + 2)], T.qh, T.sh, piece(t + 1, 0)[0], A, T.t0[:])
            send(t + 1, 0)
            merge1("S", 0)
            merge1("S", 1)
        quant(["z1"], ["qz1"], T.qz, T.sz, A, A, T.z1[:])
        for a in range(4):
            mm(["qw", "sw", "qz1"], 4 + a, T.qw, T.sw, 128 * a, T.qz, T.sz, A, A)
        if not last:
            merge1("V", 2)
            for a in range(4):
                relu(PAIR[a], ["ps%d" % (4 + a)], ["t1.%d" % a], T.t1[:, a:4 * A:4], bank(4 + a, A), 2.0 ** -5)
            merge1("S", 3)
            quant(four("t1"), ["qh%d" % (2 * t + 3)], T.qh, T.sh, piece(t + 1, 1)[0], A, T.t1[:])
            send(t + 1, 1)
            ol[1]()
            quant(four("h1"), ["q1"], T.q1, T.s1, 0, C, T.h1[:])
            mm(["qup", "sup", "q1"], 4, T.qup, T.sup, 0, T.q1, T.s1, 0, C)
            act(["ps4"], ["p1"], T.p1[:], bank(4, C))
            ol[2]()
            if first:
                quant(["vt"], ["qv"], T.qv, T.sv, 0, 128, T.vt[:])
            ol[3]()
        else:
            ol[2]()
            ol[3]()
            dma("Y", "d_out", ["olb0", "olb1", "olb2"], [], T.ol[:], T.olb[0:128:16, :])
            for a in range(4):
                relu(PAIR[a], ["ps%d" % (4 + a)], ["w2.t%d" % a], T.w2[:, W2 * a + C + A * t:W2 * (a + 1)], bank(4 + a, A), 2.0 ** -5)
            for b in range(4):
                move(PAIR[b], ["w2.l%d" % b, "w2.t%d" % b, "ls%d" % t], ["h2.%d" % b], T.h2[:, b:4 * C:4],
                     T.w2[:, W2 * b:W2 * (b + 1)].indirect(T.ls[:, LW * t + 12:LW * t + LW]))
            quant(four("h2"), ["qf"], T.qf, T.sf, 0, C, T.h2[:])
            mm(["qv", "qf"], 0, T.qv, T.sv, 0, T.qf, T.sf, 0, C)
            dma("Y", "d_out", ["qf"], [], T.oc[:], T.qf[:].bitcast(dt.uint8))
            for k in range(4):
                dma("Y" if k < 2 else "S", "d_out", ["qf"], [], T.osc[4 * k:4 * k + 4, :], T.sf[32 * k:32 * k + 4, :])
            cp(["ps0"], ["yb"], T.yb[:], bank(0, C))
            dma("S", "d_out", ["yb"], [], T.y[:], T.yb[:])

    for sem in SEMAPHORES:
        if count.get(sem, 0):
            g.wait_ge(T.sem[sem], count[sem])
